import numpy as np, ml_dtypes
CORES = [66,74,82,90,194,202,210,218]
N = 8
import mx_ref
BF = ml_dtypes.bfloat16
def entries(a):
    return np.ascontiguousarray(a.T).reshape(-1)
def table(e):
    return np.ascontiguousarray(np.reshape(e, (-1, 16)).T).astype(np.int32)
def pick(q, e):
    c = np.concatenate([q[0].reshape(128, -1, 4), np.zeros((128, 1, 4), np.uint8)], axis=1); s = np.concatenate([q[1], np.ones((16, 1), np.uint8)], axis=1)
    return (np.ascontiguousarray(c[:, e].reshape(128, -1)), np.ascontiguousarray(s[:, e]))
def join(*qs):
    return (np.concatenate([q[0] for q in qs], axis=1), np.concatenate([q[1] for q in qs], axis=1))
def put(q, e, v):
    c, s = q[0].reshape(128, -1, 4).copy(), q[1].copy(); c[:, e] = v[0].reshape(128, -1, 4); s[:, e] = v[1]
    return (c.reshape(128, -1), s)
def pk(c, s):
    return (np.ascontiguousarray(c), mx_ref.live(s))
def emit(q):
    return q[0], q[1]
def cut(t, i, w=512):
    return t[:, w * i:w * i + w]
def f(rng, *shape):
    return mx_ref.flush((rng.standard_normal(shape, dtype=np.float32) * np.exp2(rng.integers(-2, 3, shape[:-1] + (1,)))).astype(BF))
def wide(rng, *shape, cols=0):
    v = rng.standard_normal(shape, dtype=np.float32) * np.exp2(rng.integers(-12, 13, shape)).astype(np.float32)
    if cols: v *= np.repeat(np.exp2(rng.integers(-cols, cols + 1, shape[:-2] + (1, shape[-1] // 4))) * (rng.random(shape[:-2] + (1, shape[-1] // 4)) > 0.0625), 4, axis=-1).astype(np.float32)
    return mx_ref.flush(v.astype(BF))
P, K, R, LC = 128, 16, 3, 24
def near(nb):
    return np.stack([entries(nb[r]).reshape(P, 3) for r in range(N)]).astype(np.int64)
def play(x, bb, nb, u, v, a):
    n = near(nb)
    X = join(*[mx_ref.quantize(np.ascontiguousarray(x[r])) for r in range(N)])
    qu, qv = mx_ref.quantize(np.ascontiguousarray(u[0])), mx_ref.quantize(np.ascontiguousarray(v[0]))
    qa = [[mx_ref.quantize(np.ascontiguousarray(cut(a[r], i))) for i in range(4)] for r in range(N)]
    fixed = [mx_ref.matmul(qv, mx_ref.quantize(np.ascontiguousarray(bb[r])))[0] for r in range(N)]
    b = bb.astype(np.float32).reshape(N, 128, P, 4)
    done, res, made = np.zeros((N, R, K), np.int64), [], []
    for t in range(R):
        e = mx_ref.matmul(qu, X)[0]
        new = []
        for r in range(N):
            z = ((e[n[r, :, 0]] + e[n[r, :, 1]]) + e[n[r, :, 2]]) - fixed[r]
            j = np.argsort(-np.abs(z), kind="stable")[:K]
            nbs = pick(X, n[r, j].T.reshape(-1))
            s = []
            for i in range(4):
                m = mx_ref.matmul(qa[r][i], nbs)
                s.append((m[:, :K] + m[:, K:2 * K]) + m[:, 2 * K:])
            g = np.float32(0.05) * np.stack(s, axis=2) + b[r][:, j]
            new.append(mx_ref.quantize(np.ascontiguousarray(g.reshape(128, -1).astype(BF))))
            done[r, t] = j
            res.append(z)
            made.append(g)
        X = put(X, np.concatenate([P * r + done[r, t] for r in range(N)]), join(*new))
    return X, done, np.stack(res), np.stack(made)
def fit(z, g):
    top = np.abs(g.astype(BF).astype(np.float32)).reshape(-1, 16, 8, K, 4).max(axis=(2, 4))
    g = np.abs(g)
    return bool(np.isfinite(z).all() and np.isfinite(g).all() and ((g == 0) | (g >= 2.0 ** -60) & (g <= 2.0 ** 60)).all() and ((top == 0) | (top >= 2.0 ** -30) & (top <= 2.0 ** 30)).all())
def bf(v):
    return mx_ref.flush(np.asarray(v, np.float32).astype(BF))
def lone(c):
    t = np.zeros((N, 128, 512), BF)
    t[:, :, :4] = c
    return t
def few(rng, q, n, free, most):
    p = rng.permutation(free)[:most]
    return q * P + rng.permutation(np.concatenate([p, p[rng.integers(0, p.size, P)]])[:n])
def graph(rng, src=None, free=None, most=LC):
    n = np.zeros((N, P, 3), np.int64)
    if free is None: free = [np.arange(P)] * N
    for r in range(N):
        n[r, :, :2] = r * P + rng.choice(free[r], (P, 2))
        s = (r + rng.integers(1, N, P)) % N if src is None else np.full(P, src[r])
        for q in range(N):
            i = np.flatnonzero(s == q)
            n[r, i, 2] = few(rng, q, i.size, free[q], most)
    return n
def stored(n):
    return np.stack([table(n[r].reshape(-1)) for r in range(N)])
def setup_inputs(rng):
    return {"x": f(rng, N, 128, 4 * P), "bb": f(rng, N, 128, 4 * P), "nb": stored(graph(rng)), "u": lone(f(rng, 128, 4)), "v": lone(f(rng, 128, 4)),
            "a": bf(f(rng, N, 128, 2048).astype(np.float32) * np.float32(2.0 ** -4)), "w": f(rng, N, 128, 512)}
def signs(rng):
    return 1.0 - 2.0 * rng.integers(0, 2, (128, 4))
def signed(rng, sg, size):
    return bf(((1 + rng.random((N, 128, P, 4))) * size[:, None, :, None] * sg[:, None, :] + 0.0).reshape(N, 128, 4 * P))
def single(rng, sg, size):
    return lone(bf((1 + rng.random((128, 4))) * sg * size))
def setup_inputs_again(rng):
    d, sg, size, m = setup_inputs(rng), signs(rng), np.zeros((N, P)), K // 8
    o = np.stack([rng.permutation(P) for r in range(N)])
    rest = np.sort(o[:, 7 * m:], axis=1)
    hold = np.stack([rng.permutation(rest[r, -5:]) for r in range(N)])
    n = graph(rng, free=rest[:, :-5], most=LC - 2)
    large, small = (1 + rng.random((128, 4))) * sg * 2.0 ** 20, (1 + rng.random((128, 4))) * sg * 2.0 ** -8
    top = np.arange(128)[:, None] < 64
    five = np.stack([large * top, large * ~top, -large, large, small], axis=1) + 0.0
    x = np.zeros((N, 128, P, 4))
    for r in range(N):
        x[r][:, hold[r]] = five
        h, left, both, alone = o[r, :4 * m], o[r, 4 * m:5 * m], o[r, 5 * m:6 * m], o[r, 6 * m:7 * m]
        size[r, h] = 64
        size[r, left] = 64
        n[r, h, 0] = r * P + rng.permutation(h)
        n[r, left, 0], n[r, left, 1] = r * P + hold[r, 0], r * P + hold[r, 1]
        n[r, both, 0], n[r, both, 1] = r * P + hold[r, 3], r * P + hold[r, 2]
        for i, k in ((left, 2), (both, 4), (alone, 4)):
            q = n[r, i, 2] // P
            n[r, i, 2] = q * P + hold[q, k]
    bb = signed(rng, sg, size).reshape(N, 128, P, 4)
    for r in range(N): bb[r][8:, o[r, 4 * m:5 * m]] = 0
    d.update(x=bf(x.reshape(N, 128, 4 * P)), bb=bb.reshape(N, 128, 4 * P), nb=stored(n), u=single(rng, sg, 1.0), v=single(rng, sg, 4.0))
    return d
def setup_inputs_far(rng):
    h = int(rng.integers(0, N))
    src = np.full(N, h)
    src[h] = (h + int(rng.integers(1, N))) % N
    d, n, sg, size = setup_inputs(rng), graph(rng, src), signs(rng), np.full((N, P), 2.0 ** 20)
    for r in range(N):
        first = np.unique(n[r, :, 2], return_index=True)[1]
        size[r, rng.permutation(first)[:K]] = 2.0 ** 26
    d.update(x=signed(rng, sg, np.full((N, P), 2.0 ** 20)), bb=signed(rng, sg, size), nb=stored(n), u=single(rng, sg, 2.0 ** 23), v=single(rng, sg, 2.0 ** 29))
    return d
def setup_inputs_moved(rng):
    d, n, sg, size = setup_inputs(rng), np.zeros((N, P, 3), np.int64), signs(rng), np.full((N, P), 2.0 ** -4)
    o = [rng.permutation(P) for r in range(N)]
    for r in range(N):
        size[r, o[r][:K]] = 64
        n[r, :, :2] = r * P + rng.choice(o[r][K:], (P, 2))
        m = np.zeros(P, bool)
        m[rng.permutation(P)[:K + K // 2]] = True
        s = (r + rng.integers(1, N, P)) % N
        for q in range(N):
            hot, cold = rng.permutation(o[q][:K])[:LC // 2], rng.permutation(o[q][K:])[:LC - LC // 2]
            i, k = np.flatnonzero((s == q) & m), np.flatnonzero((s == q) & ~m)
            n[r, i, 2] = q * P + rng.choice(hot, i.size)
            n[r, k, 2] = q * P + rng.choice(cold, k.size)
    d.update(x=signed(rng, sg, np.full((N, P), 2.0 ** -6)), bb=signed(rng, sg, size), nb=stored(n), u=single(rng, sg, 16.0), v=single(rng, sg, 1.0))
    return d
def setup_inputs_spread(rng):
    d = setup_inputs(rng)
    d["x"] = wide(rng, N, 128, 4 * P, cols=4)
    d["bb"] = wide(rng, N, 128, 4 * P, cols=4)
    return d
def setup_inputs_ties(rng):
    d, n = setup_inputs(rng), np.zeros((N, P, 3), np.int64)
    kind = np.stack([rng.permutation(np.arange(P) % 4) for r in range(N)])
    for k in ("x", "bb"):
        c = f(rng, 128, 8).astype(np.float32).reshape(128, 2, 4)
        d[k] = np.stack([bf((c[:, kind[r] >> 1] * (1 - 2 * (kind[r] & 1))[None, :, None]).reshape(128, -1)) for r in range(N)])
    for r in range(N):
        s = (r + rng.integers(1, N, P)) % N
        for k in range(4):
            i = np.flatnonzero(kind[r] == k)
            n[r, i, 0] = r * P + rng.choice(i, i.size)
            n[r, i, 1] = r * P + rng.choice(np.flatnonzero(kind[r] == (k ^ 2)), i.size)
            for q in range(N):
                j = i[s[i] == q]
                n[r, j, 2] = q * P + rng.choice(rng.permutation(np.flatnonzero(kind[q] == k))[:LC // 4], j.size)
    d["nb"] = stored(n)
    return d
def check_inputs(d):
    b = []
    for k in ("x", "bb", "u", "v", "a", "w"):
        t = np.abs(d[k].astype(np.float32))
        if not (np.isfinite(t).all() and ((t == 0) | (t >= 2.0 ** -30) & (t <= 2.0 ** 30)).all()): b.append("a value of " + k)
    for k in ("u", "v"):
        t = d[k].astype(np.float32)
        if (t[:, :, 4:] != 0).any(): b.append(k + " has numbers behind its column 0")
        if (t != t[:1]).any(): b.append(k + " isn't the same on all ranks")
    n = near(d["nb"])
    at, own = n // P, np.arange(N)[:, None, None]
    if n.min() < 0 or n.max() >= N * P or (at[:, :, :2] != own).any() or (at[:, :, 2] == own[:, :, 0]).any(): b.append("nb")
    elif any(np.unique(n[r, :, 2][at[r, :, 2] == q]).size > LC for r in range(N) for q in range(N)): b.append("nb names too many columns of one rank")
    if not b:
        try:
            with np.errstate(all="ignore"):
                X, done, z, g = play(d["x"], d["bb"], d["nb"], d["u"], d["v"], d["a"])
                good = fit(z, g)
        except Exception:
            good = False
        if not good: b.append("a number that the rounds make")
    return b
def reference(x, bb, nb, u, v, a, w):
    X, done, z, g = play(x, bb, nb, u, v, a)
    oc, osc, y = np.zeros((N, 128, 4 * P), np.uint8), np.zeros((N, 16, P), np.uint8), np.zeros((N, 128, P), np.float32)
    for r in range(N):
        q = pick(X, np.arange(P * r, P * r + P))
        oc[r], osc[r] = emit(q)
        y[r] = mx_ref.matmul(mx_ref.quantize(np.ascontiguousarray(w[r])), q)
    return {"oc": oc, "osc": osc, "nd": done.astype(np.float32), "y": y}

@@ -1,0 +1,469 @@
+import numpy as np
+from concourse.bass import DstId, RemoteDMATransfer
+from concourse.mybir import dt, AluOpType, AxisListType, ActivationFunctionType
+
+F32, I32, U16, B16, Q8, U8 = "float32", "int32", "uint16", "bfloat16", "float8_e4m3fn_x4", "uint8"
+P, K, R, LC, SLOT = 128, 16, 3, 24, 32
+SCRATCH = {}
+ALIAS = {}
+
+
+def _sb(kind, **names):
+    for k in names:
+        SCRATCH[k] = ("sbuf", [128, names[k]], kind)
+
+
+def _pack(kind, big, **names):
+    at = 0
+    for k in names:
+        ALIAS[k] = (big, at, names[k])
+        at += (names[k] + 7) // 8 * 8
+    SCRATCH[big] = ("sbuf", [128, at], kind)
+
+
+_pack(I32, "KI", PID=1, PM16i=1, PM32i=1, PM4i=1, W1=1, W2=1, IO16=32, OFFC=8, MJ=8, MJ2=8, MJ3=8, MJ4=8)
+_pack(F32, "KF", PM16=1, PM32=1, PM4=1, RM3=1, W3=1, MH=3, CI=8, FA=8, FB=8, FC=8, FD0=8, FO=8, GO1=8, GO=8, NGO=8, RS=8, RV=8,
+      TAU=14, NTAU=14, PSC=14, PVC=14, R3=1, LA1=1, LA2=1, LAB=4, CT=4, IX=1)
+_pack(U16, "KU", FOU=8, RU=8, PU=28, NBU=24, CN=48, CIO=16, LN=16, NLD=32, FLD=16, LF=8, IDD=16, OFF8=8, PL=4, BO=8, JU=2, UO=32,
+      LFIN=8)
+_sb(I32, NB=24, IOT=1024, KJ=512, FRI=128, SF=144, SFL=144, AB=136)
+_sb(F32, GR1=128, GR=128, JK=128, CMR=384, SAME=128, NEQ=128, SLT=128, KB=128, KAP=128, CMP=640, RLD=448, RLT=448,
+    PIO=128, NBR=384, D3=768, POS=1024, PT=512, FT=256, NP=128, UPD=1024, UG=256, LT=256, CK1=512, CK=512,
+    NZ=128, RW=128, TR=128, SP=512, CM=512, JK4=512, MM=128, MT=128, GP=128, GPT=128, CC=128, T1=64, T2=64, T3=64,
+    NDB=48, FPD=256, FPT=256, YS=128)
+_sb(U16, RQ=14, RQIN=14, GL0=2, GL1=2, RI0=8, RI1=8)
+_sb(B16, xb=512, bbb=512, ub=16, vb=16, ab=2048, wb=512, UT=512, VT=512, XT=512, BG=64)
+for _n, _w in (("XQ", 128), ("NW", 512), ("BBQ", 128), ("UQ", 128), ("VQ", 128), ("AQ", 512), ("WQ", 128), ("SL", 224), ("FW", 512),
+               ("PZ", 384), ("PX", 128), ("FIN", 128)):
+    SCRATCH[_n] = ("sbuf", [128, _w], Q8)
+    SCRATCH[_n + "S"] = ("sbuf", [128, _w], U8)
+BANKS = ("Z", "S0", "S1", "S2", "S3", "Y")
+for _n in BANKS:
+    SCRATCH[_n] = ("psum", [128, 512], F32)
+SEMAPHORES = ["cv", "cs", "ct", "cp", "ln0", "ln1", "lx", "lb", "lu", "lv", "la", "lw", "rq", "rc", "rs", "loc",
+              "li0", "li1", "cd0", "cd1", "sc0", "sc1", "on", "oc", "os", "oy"]
+
+
+def rank_program(g, core, T, topo):
+    me = T.rank_of(core)
+    if me is None:
+        return
+    n = len(T.cores)
+    OP, FN, AX = AluOpType, ActivationFunctionType, AxisListType.X
+    E = {"v": g.vector, "s": g.scalar, "t": g.tensor, "p": g, "y": g.sync}
+    SEM = {"v": "cv", "s": "cs", "t": "ct", "p": "cp"}
+    clock = {e: {} for e in E}
+    total, recs = {}, {}
+
+    def norm(x):
+        return (x[0], 0, 512, 1) if x[0] in BANKS else x
+
+    def meet(a, b):
+        if a[1] >= b[2] or b[1] >= a[2]:
+            return False
+        return not (a[3] == b[3] and a[3] > 1 and (a[1] - b[1]) % a[3])
+
+    def sync(e, reads, writes):
+        toks = []
+        for kind, xs in (("r", reads), ("w", writes)):
+            for x in xs:
+                x = norm(x)
+                bank = x[0] in BANKS
+                for (y, k, tok, by) in recs.get(x[0], []):
+                    if bank and by == e == "t":
+                        continue
+                    if (kind == "w" or k == "w" or (bank and by != e)) and meet(x, y):
+                        toks.append(tok)
+        best = {}
+        for t in toks:
+            if clock[e].get(t[0], 0) < t[1] and best.get(t[0], (0, 0))[1] < t[1]:
+                best[t[0]] = t
+        for s in sorted(best):
+            t = best[s]
+            if any(o != s and best[o][2].get(s, 0) >= t[1] for o in best):
+                continue
+            E[e].wait_ge(T.sem[s], t[1])
+        for s in best:
+            for k in best[s][2]:
+                clock[e][k] = max(clock[e].get(k, 0), best[s][2][k])
+            clock[e][s] = max(clock[e].get(s, 0), best[s][1])
+
+    def note(e, tok, reads, writes):
+        for x in writes:
+            x = norm(x)
+            old = recs.setdefault(x[0], [])
+            if x[3] == 1 and x[0] not in BANKS:
+                old[:] = [r for r in old if not (x[1] <= r[0][1] and r[0][2] <= x[2])]
+            old.append((x, "w", tok, e))
+        for x in reads:
+            x = norm(x)
+            recs.setdefault(x[0], []).append((x, "r", tok, e))
+
+    def emit(e, fn, reads, writes):
+        reads = [x for x in reads if isinstance(x, tuple)]
+        sync(e, reads, writes)
+        s = SEM[e]
+        total[s] = total.get(s, 0) + 1
+        fn().then_inc(T.sem[s], 1)
+        snap = dict(clock[e])
+        snap[s] = total[s]
+        note(e, (s, total[s], snap), reads, writes)
+
+    def dma(q, s, pairs, reads, writes):
+        sync(q, reads, writes)
+        for o, i in pairs:
+            E[q].dma_start(o, i).then_inc(T.sem[s], 16)
+        total[s] = 16 * len(pairs)
+        snap = dict(clock[q])
+        snap[s] = total[s]
+        note("d", (s, total[s], snap), reads, writes)
+
+    def arrive(s, val, writes):
+        total[s] = val
+        note("r", (s, val, {s: val}), [], writes)
+
+    def X(name, lo=0, hi=None, st=1):
+        if name in ALIAS:
+            big, at, w = ALIAS[name]
+            return (big, at + lo, at + (w if hi is None else hi), st)
+        return (name, lo, SCRATCH[name][1][1] if hi is None else hi, st)
+
+    def ap(x):
+        if not isinstance(x, tuple):
+            return x
+        return T[x[0]][:, x[1]:x[2]] if x[3] == 1 else T[x[0]][:, x[1]:x[2]:x[3]]
+
+    def sc(x):
+        return (x[0] + "S", x[1], x[2], x[3])
+
+    def tt(o, a, b, op):
+        emit("v", lambda: g.vector.tensor_tensor(ap(o), ap(a), ap(b), op), [a, b], [o])
+
+    def ts(o, a, s1, op0, s2=None, op1=None):
+        if op1 is None:
+            emit("v", lambda: g.vector.tensor_scalar(ap(o), ap(a), ap(s1), None, op0), [a, s1], [o])
+        else:
+            emit("v", lambda: g.vector.tensor_scalar(ap(o), ap(a), ap(s1), ap(s2), op0, op1), [a, s1, s2], [o])
+
+    def tc(o, a):
+        emit("v", lambda: g.vector.tensor_copy(ap(o), ap(a)), [a], [o])
+
+    def tr(o, a):
+        emit("v", lambda: g.vector.transpose(ap(o), ap(a)), [a], [o])
+
+    def red(o, a):
+        emit("v", lambda: g.vector.tensor_reduce(ap(o), ap(a), AX, OP.add), [a], [o])
+
+    def fill(o, c):
+        emit("v", lambda: g.vector.memset(ap(o), c), [], [o])
+
+    def gat(o, win, off):
+        emit("v", lambda: g.vector.tensor_copy(ap(o), ap(win).indirect(ap(off))), [win, off], [o])
+
+    def sct(win, off, a):
+        emit("v", lambda: g.vector.tensor_copy(ap(win).indirect(ap(off)), ap(a)), [a, off], [win])
+
+    def act(o, a, f, bias=None, scale=None, acc=None, off=None):
+        kw = {}
+        if bias is not None:
+            kw["bias"] = ap(bias)
+        if scale is not None:
+            kw["scale"] = ap(scale)
+        if acc is not None:
+            kw["accum_out"] = ap(acc)
+
+        def go():
+            return g.scalar.activation(ap(o), ap(a) if off is None else ap(a).indirect(ap(off)), f, **kw)
+        emit("s", go, [a, bias, scale, off], [o] + ([acc] if acc is not None else []))
+
+    def quant(o, tile):
+        emit("v", lambda: g.vector.quantize_mx(ap(o), ap(sc(o)), ap(tile)), [tile], [o, sc(o)])
+
+    def pick(o, win, off):
+        emit("v", lambda: g.vector.tensor_copy(ap(o).bitcast(dt.uint32), ap(win).bitcast(dt.uint32).indirect(ap(off))),
+             [win, off], [o])
+        emit("s", lambda: g.scalar.activation(ap(sc(o)), ap(sc(win)).indirect(ap(off)), FN.Copy), [sc(win), off], [sc(o)])
+
+    def mm(bank, a, b, start=True, stop=True):
+        o = (bank, 0, b[2] - b[1], 1)
+        emit("t", lambda: g.tensor.matmul_mx(ap(o), ap(a), ap(sc(a)), ap(b), ap(sc(b)), start, stop),
+             [a, sc(a), b, sc(b)], [o])
+
+    def iota(o, pattern, cm=0):
+        emit("p", lambda: g.iota(ap(o), pattern, 0, cm), [], [o])
+
+    peers = [(me + 1 + i) % n for i in range(n - 1)]
+
+    def slot_at(s):
+        return (me - s - 1) % n
+
+    def dst(s):
+        rid, pid = topo.addr(T.cores[s], core)
+        return DstId(rid=rid, pnc=pid)
+
+    shared = topo.mask(core, T.cores[peers[0]])
+    for s in peers:
+        shared &= topo.mask(core, T.cores[s])
+
+    def bits(m):
+        return bin(m).count("1")
+
+    def each(srcs, dsts, sem, reads):
+        sync("p", reads, [])
+        trs = []
+        for i, s in enumerate(peers):
+            m = 1 << topo.engines(core, T.cores[s])[i]
+            trs.append(RemoteDMATransfer(dst_ids=[dst(s)], dma_engine_mask=m, remote_sem=T.sem[sem], src=srcs[i], dst=dsts[i]))
+        total["loc"] = total.get("loc", 0) + len(trs)
+        g.remote_dma_fused(trs, local_sem=T.sem.loc)
+
+    def spread(src, dsts, sem, reads):
+        sync("p", reads, [])
+        total["loc"] = total.get("loc", 0) + bits(shared)
+        g.remote_dma_fused([RemoteDMATransfer(dst_ids=[dst(s) for s in peers], dma_engine_mask=shared, remote_sem=T.sem[sem],
+                                              srcs=[src], dsts=dsts)], local_sem=T.sem.loc)
+
+    u8 = dt.uint8
+
+    for q, s, lo in (("y", "ln0", 0), ("s", "ln1", 4)):
+        for k in range(lo, lo + 4):
+            E[q].dma_start(T.NB[16 * k:16 * k + 16, :], T.nb[:]).then_inc(T.sem[s], 16)
+        total[s] = 64
+    recs["NB"] = [(X("NB"), "w", (s, 64, {s: 64}), "d") for s in ("ln0", "ln1")]
+    dma("y", "lx", [(T.xb[:], T.x[:])], [], [X("xb")])
+    dma("s", "lu", [(T.ub[:], T.u[:, 0:16])], [], [X("ub")])
+    dma("s", "lv", [(T.vb[:], T.v[:, 0:16])], [], [X("vb")])
+    dma("y", "lb", [(T.bbb[:], T.bb[:])], [], [X("bbb")])
+    dma("y", "la", [(T.ab[:], T.a[:])], [], [X("ab")])
+    dma("y", "lw", [(T.wb[:], T.w[:])], [], [X("wb")])
+
+    iota(X("PID"), [[0, 1]], 1)
+    iota(X("IOT"), [[1, 1024]])
+    iota(X("OFFC"), [[256, 4], [0, 2]])
+    iota(X("KJ"), [[-32, 4], [1, 128]])
+    emit("p", lambda: g.iota(ap(X("POS", 768, 1024)), [[64, 8], [0, 2], [4, 16]], 0, 0, allow_small_or_imprecise_dtypes=True),
+         [], [X("POS", 768, 1024)])
+    for m, k in (("PM16", 15), ("PM32", 31), ("PM4", 3)):
+        ts(X(m + "i"), X("PID"), k, OP.bitwise_and)
+        tc(X(m), X(m + "i"))
+    ts(X("W1"), X("PM16i"), 11, OP.mult)
+    ts(X("W2"), X("W1"), 5, OP.arith_shift_right)
+    ts(X("W3"), X("W2"), -3.0, OP.mult)
+    tt(X("RM3"), X("W3"), X("PM16"), OP.add)
+    for h in range(3):
+        ts(X("MH", h, h + 1), X("RM3"), float(2 - h), OP.is_equal)
+    fill(X("SF", 0, 8), -1)
+    fill(X("SF", 8, 144), 0)
+
+    for h, o in enumerate(("FA", "FB", "FC")):
+        ts(X(o), X("NB", h, 24, 3), X("MH", h, h + 1), OP.mult)
+    tt(X("FD0"), X("FA"), X("FB"), OP.add)
+    tt(X("FO"), X("FD0"), X("FC"), OP.add)
+    tc(X("FOU"), X("FO"))
+    gat(X("FRI"), X("IOT"), X("FOU"))
+    ts(X("CI"), X("IOT", 0, 128, 16), X("PM16"), OP.add)
+    ts(X("GO1"), X("FO"), 128.0, OP.mult)
+    ts(X("GR1"), X("FRI"), 128.0, OP.mult)
+    tt(X("GO"), X("GO1"), X("CI"), OP.add)
+    tt(X("GR"), X("GR1"), X("IOT", 0, 128), OP.add)
+    ts(X("NGO"), X("GO"), -1.0, OP.mult)
+    NS = 5
+    for t in range(NS):
+        act(X("JK"), X("GR"), FN.Sign, bias=X("NGO", t, t + 1), acc=X("RS", t, t + 1))
+    for t in range(NS, 8):
+        ts(X("CMR", 128 * (t - NS), 128 * (t - NS) + 128), X("GR"), X("GO", t, t + 1), OP.is_lt)
+    for t in range(NS, 8):
+        red(X("RV", t, t + 1), X("CMR", 128 * (t - NS), 128 * (t - NS) + 128))
+    tc(X("RU", NS, 8), X("RV", NS, 8))
+    cut = 2 * (n - 1 - me)
+    if me < n - 1:
+        ts(X("TAU", 0, cut), X("IOT", SLOT * (me + 1), SLOT * n, 16), X("PM16"), OP.add)
+    if me > 0:
+        ts(X("TAU", cut, 14), X("IOT", 0, SLOT * me, 16), X("PM16"), OP.add)
+    ts(X("NTAU"), X("TAU"), -1.0, OP.mult, 0.5, OP.add)
+    ts(X("RU", 0, NS), X("RS", 0, NS), -0.5, OP.mult, 63.5, OP.add)
+    sct(X("SF", 8, 136), X("RU"), X("FRI"))
+    ts(X("AB", 7, 136), X("SF", 7, 136), 896, OP.bitwise_and)
+    tt(X("NEQ"), X("SF", 8, 136), X("SF", 7, 135), OP.not_equal)
+    tt(X("SAME"), X("AB", 8, 136), X("AB", 7, 135), OP.is_equal)
+    ts(X("KB"), X("AB", 8, 136), 0.25, OP.mult, -1.0, OP.add)
+    emit("v", lambda: g.vector.tensor_tensor_scan(ap(X("SLT")), ap(X("SAME")), ap(X("NEQ")), 0.0, OP.mult, OP.add),
+         [X("SAME"), X("NEQ")], [X("SLT")])
+    tt(X("KAP"), X("KB"), X("SLT"), OP.add)
+    NT = 9
+    for c in range(NT):
+        act(X("JK"), X("KAP"), FN.Sign, bias=X("NTAU", c, c + 1), acc=X("PSC", c, c + 1))
+    for c in range(NT, 14):
+        ts(X("CMP", 128 * (c - NT), 128 * (c - NT) + 128), X("KAP"), X("TAU", c, c + 1), OP.is_lt)
+    for c in range(NT, 14):
+        red(X("PVC", c, c + 1), X("CMP", 128 * (c - NT), 128 * (c - NT) + 128))
+    ts(X("SFL", 8, 144), X("SF", 8, 144), 127, OP.bitwise_and)
+    for d in range(2):
+        tc(X("PU", 2 * NT + d, 28, 2), X("PVC", NT, 14))
+    for d in range(2):
+        ts(X("PU", d, 2 * NT, 2), X("PSC", 0, NT), -0.5, OP.mult, 64.0, OP.add)
+    gat(X("RLD"), X("SFL", 8, 144), X("PU"))
+    tr(X("RLT"), X("RLD"))
+    tc(X("RQ"), X("RLT", 0, 448, 32))
+    each([T.RQ[:, 2 * i:2 * i + 2] for i in range(n - 1)],
+         [T.RQIN[:, 2 * slot_at(s):2 * slot_at(s) + 2] for s in peers], "rq", [X("RQ")])
+
+    quant(X("XQ"), X("xb"))
+    quant(X("NW", 0, 128), X("xb"))
+    ts(X("UO"), X("IOT", 0, 32), 0.0, OP.mult, X("PM4"), OP.add)
+    act(X("UT"), X("ub"), FN.Copy, off=X("UO"))
+    act(X("VT"), X("vb"), FN.Copy, scale=-1.0, off=X("UO"))
+    tc(X("NBU"), X("NB"))
+    gat(X("NBR"), X("IOT"), X("NBU"))
+    ts(X("R3"), X("PM16"), 3.0, OP.mult)
+    for k in range(3):
+        for d in range(2):
+            ts(X("CN", 16 * k + d, 16 * k + 16, 2), X("IOT", k, 384, 48), X("R3"), OP.add)
+    act(X("D3"), X("NBR"), FN.Copy, off=X("CN"))
+    quant(X("UQ"), X("UT"))
+    quant(X("VQ"), X("VT"))
+    quant(X("BBQ"), X("bbb"))
+
+    arrive("rq", n - 1, [X("RQIN")])
+    pick(X("SL"), X("XQ"), X("RQIN"))
+    blocks = [(SLOT * i, SLOT * i + LC) for i in range(n - 1)]
+    land = (SLOT * me, SLOT * me + LC)
+    each([T.SL[:, a:b].bitcast(u8) for a, b in blocks], [T.FW[:, land[0]:land[1]].bitcast(u8) for s in peers], "rc", [X("SL")])
+    each([T.SLS[:, a:b] for a, b in blocks], [T.FWS[:, land[0]:land[1]] for s in peers], "rs", [X("SLS")])
+    arrive("rc", n - 1, [X("FW", 0, 256)])
+    arrive("rs", n - 1, [X("FWS", 0, 256)])
+
+    ts(X("POS", 0, 512), X("D3", 0, 512), float(-P * me), OP.add)
+    tr(X("PT"), X("POS", 0, 512))
+    tc(X("LN"), X("PT", 0, 512, 32))
+
+    def near_sums():
+        pick(X("PZ", 0, 256), X("NW"), X("LN"))
+        mm("Z", X("UQ"), X("PZ", 0, 128), True, False)
+        mm("Z", X("UQ"), X("PZ", 128, 256), False, False)
+    near_sums()
+    ts(X("MJ"), X("IOT", 2, 384, 48), X("R3"), OP.add)
+    ts(X("MJ2"), X("MJ"), 4, OP.arith_shift_right)
+    ts(X("MJ3"), X("MJ2"), 171, OP.mult)
+    ts(X("MJ4"), X("MJ3"), 9, OP.arith_shift_right)
+    ts(X("MJ2"), X("MJ"), 15, OP.bitwise_and)
+    ts(X("MJ3"), X("MJ4"), 16, OP.mult)
+    for d in range(2):
+        tt(X("LT", 8 * d, 8 * d + 8), X("MJ2"), X("MJ3"), OP.add)
+        tc(X("CIO", d, 16, 2), X("LT", 8 * d, 8 * d + 8))
+    gat(X("PIO"), X("KAP"), X("RU"))
+    gat(X("POS", 512, 768), X("PIO"), X("CIO"))
+    tr(X("FT"), X("POS", 512, 768))
+    tc(X("LF"), X("FT", 0, 256, 32))
+    ts(X("CK1"), X("KJ"), X("PM32"), OP.is_lt, -2.0 ** -24, OP.mult)
+    ts(X("CK"), X("CK1"), 1.0, OP.add)
+    ts(X("LA1"), X("PM32"), 16.0, OP.is_ge, 16.0, OP.mult)
+    tt(X("LA2"), X("LA1"), X("PM32"), OP.add)
+    ts(X("LAB"), X("IOT", 0, 256, 64), X("LA2"), OP.add)
+    ts(X("IO16"), X("IOT", 0, 32), 15, OP.bitwise_and)
+    for b in range(4):
+        quant(X("AQ", 128 * b, 128 * b + 128), X("ab", 512 * b, 512 * b + 512))
+    quant(X("PX"), X("xb"))
+    fill(X("XT"), 0.0)
+
+    c05 = float(np.float32(0.05))
+    TINY = 2.0 ** -100
+    for t in range(R):
+        fw = (256, 384, 512)[t]
+        pick(X("PZ", 256, 384), X("FW", 0, fw), X("LF"))
+        mm("Z", X("UQ"), X("PZ", 256, 384), False, False)
+        mm("Z", X("VQ"), X("BBQ"), False, True)
+        z = X("Z", 0, 128)
+        ts(X("NZ"), z, -1.0, OP.mult, TINY, OP.max)
+        tt(X("RW"), z, X("NZ"), OP.max)
+        tr(X("TR"), X("RW"))
+        for k in range(4):
+            act(X("SP", 128 * k, 128 * k + 128), X("CK", 128 * k, 128 * k + 128), FN.Identity, scale=X("TR", 32 * k, 32 * k + 1))
+        for k in range(4):
+            c = X("CM", 128 * k, 128 * k + 128)
+            tt(c, X("RW"), X("SP", 128 * k, 128 * k + 128), OP.is_gt)
+            act(X("JK4", 128 * k, 128 * k + 128), c, FN.Identity, acc=X("CT", k, k + 1))
+        for k in range(4):
+            ts(X("MM", 32 * k, 32 * k + 32), X("IO16"), X("CT", k, k + 1), OP.is_equal, X("LAB", k, k + 1), OP.mult)
+        tr(X("MT"), X("MM"))
+        red(X("IX"), X("MT"))
+        ts(X("OFF8"), X("OFFC"), X("IX"), OP.add)
+        gat(X("GP"), X("POS"), X("OFF8"))
+        tr(X("GPT"), X("GP"))
+        tc(X("PL"), X("GPT", 0, 128, 32))
+        pick(X("PX", 0, 32), X("NW", 0, 128 * (t + 1)), X("PL", 0, 2))
+        pick(X("PX", 32, 48), X("FW", 0, fw), X("PL", 2, 3))
+        for b in range(4):
+            mm("S%d" % b, X("AQ", 128 * b, 128 * b + 128), X("PX"))
+        j4 = X("GPT", 96, 97)
+        gl = "GL%d" % t
+        if t < R - 1:
+            ts(X(gl, 0, 1), j4, 0.25, OP.mult, float(P * me), OP.add)
+            spread(T[gl][:, 0:1], [T["RI%d" % t][:, slot_at(s):slot_at(s) + 1] for s in peers], "li%d" % t, [X(gl, 0, 1)])
+        ts(X("BO", 0, 8, 2), X("IOT", 0, 4), j4, OP.add)
+        ts(X("JU", 0, 1), j4, 0.25, OP.mult)
+        for b in range(4):
+            act(X("BG", b, 64, 4), X("bbb"), FN.Copy, off=X("BO", 2 * b, 2 * b + 1))
+        if t == 0:
+            tc(X("NP"), X("IOT", 0, 128))
+
+        def moved():
+            sct(X("NP"), X("JU", 0, 1), X("IOT", P * (t + 1), P * (t + 1) + K))
+        if t == R - 1:
+            moved()
+            for d in range(2):
+                tc(X("IDD", d, 16, 2), X("CI"))
+            gat(X("FPD"), X("NP"), X("IDD"))
+            tr(X("FPT"), X("FPD"))
+            tc(X("LFIN"), X("FPT", 0, 256, 32))
+        for b in range(4):
+            act(X("CC", 32 * b, 32 * b + 32), X("S%d" % b, 16, 48), FN.Copy)
+            tt(X("T1", b, 64, 4), X("S%d" % b, 0, 16), X("CC", 32 * b, 32 * b + 16), OP.add)
+        for b in range(4):
+            tt(X("T2", b, 64, 4), X("T1", b, 64, 4), X("CC", 32 * b + 16, 32 * b + 32), OP.add)
+        ts(X("T3"), X("T2"), c05, OP.mult)
+        tt(X("XT", 0, 64), X("T3"), X("BG"), OP.add)
+        new = P * (t + 1)
+        quant(X("NW", new, new + 128), X("XT"))
+        if t < R - 1:
+            spread(T.NW[:, new:new + K].bitcast(u8),
+                   [T.FW[:, fw + K * slot_at(s):fw + K * slot_at(s) + K].bitcast(u8) for s in peers], "cd%d" % t, [X("NW", new, new + K)])
+            spread(T.NWS[:, new:new + K],
+                   [T.FWS[:, fw + K * slot_at(s):fw + K * slot_at(s) + K] for s in peers], "sc%d" % t, [X("NWS", new, new + K)])
+            emit("v", lambda: g.vector.tensor_scalar(T.NDB[0:1, K * t:K * t + K], T.GP[0:1, 96:112], 0.25, None, OP.mult),
+                 [X("GP")], [X("NDB", K * t, K * t + K)])
+            moved()
+            if t == 0:
+                for d in range(2):
+                    tc(X("NLD", d, 32, 2), X("LN"))
+                tr(X("LT"), X("D3", 512, 768))
+                for d in range(2):
+                    tc(X("FLD", d, 16, 2), X("LT", 0, 256, 32))
+                fill(X("UPD"), 0.0)
+            gat(X("POS", 0, 512), X("NP"), X("NLD"))
+            tr(X("PT"), X("POS", 0, 512))
+            tc(X("LN"), X("PT", 0, 512, 32))
+            near_sums()
+            arrive("li%d" % t, (n - 1) * bits(shared), [X("RI%d" % t, 0, 7)])
+            sct(X("UPD"), X("RI%d" % t, 0, 7), X("IOT", fw, fw + 112))
+            gat(X("UG"), X("UPD"), X("FLD"))
+            tt(X("POS", 512, 768), X("POS", 512, 768), X("UG"), OP.max)
+            tr(X("FT"), X("POS", 512, 768))
+            tc(X("LF"), X("FT", 0, 256, 32))
+            if t == 0:
+                quant(X("WQ"), X("wb"))
+            arrive("cd%d" % t, (n - 1) * bits(shared), [X("FW", fw, fw + 112)])
+            arrive("sc%d" % t, (n - 1) * bits(shared), [X("FWS", fw, fw + 112)])
+        else:
+            pick(X("FIN"), X("NW"), X("LFIN"))
+            mm("Y", X("WQ"), X("FIN"))
+            dma("y", "oc", [(T.oc[:], T.FIN[:].bitcast(u8))], [X("FIN")], [])
+            dma("y", "os", [(T.osc[4 * k:4 * k + 4, :], T.FINS[32 * k:32 * k + 4, :]) for k in range(4)], [X("FINS")], [])
+            tc(X("YS"), X("Y", 0, 128))
+            dma("s", "oy", [(T.y[:], T.YS[:])], [X("YS")], [])
+            emit("v", lambda: g.vector.tensor_scalar(T.NDB[0:1, K * t:K * t + K], T.GP[0:1, 96:112], 0.25, None, OP.mult),
+                 [X("GP")], [X("NDB", K * t, K * t + K)])
+            dma("s", "on", [(T.nd[:], T.NDB[0:1, :])], [X("NDB")], [])
+    for s in total:
+        if clock["p"].get(s, 0) < total[s]:
+            g.wait_ge(T.sem[s], total[s])

@@ -3,7 +3,7 @@ from concourse.bass import DstId, RemoteDMATransfer
 from concourse.mybir import dt, AluOpType, AxisListType, ActivationFunctionType
 
 F32, I32, U16, B16, Q8, U8 = "float32", "int32", "uint16", "bfloat16", "float8_e4m3fn_x4", "uint8"
-P, K, R, LC, SLOT = 128, 16, 3, 24, 32
+P, K, R, LC = 128, 16, 3, 24
 SCRATCH = {}
 ALIAS = {}
 
@@ -21,19 +21,19 @@ def _pack(kind, big, **names):
     SCRATCH[big] = ("sbuf", [128, at], kind)
 
 
-_pack(I32, "KI", PID=1, PM16i=1, PM32i=1, PM4i=1, W1=1, W2=1, IO16=32, OFFC=8, MJ=8, MJ2=8, MJ3=8, MJ4=8)
-_pack(F32, "KF", PM16=1, PM32=1, PM4=1, RM3=1, W3=1, MH=3, CI=8, FA=8, FB=8, FC=8, FD0=8, FO=8, GO1=8, GO=8, NGO=8, RS=8, RV=8,
-      TAU=14, NTAU=14, PSC=14, PVC=14, R3=1, LA1=1, LA2=1, LAB=4, CT=4, IX=1)
-_pack(U16, "KU", FOU=8, RU=8, PU=28, NBU=24, CN=48, CIO=16, LN=16, NLD=32, FLD=16, LF=8, IDD=16, OFF8=8, PL=4, BO=8, JU=2, UO=32,
+_pack(I32, "KI", PID=1, PM16i=1, PM32i=1, PM4i=1, W1=1, W2=1, IO16=32, OFFC=8, MJ=16, MJ2=16, MJ3=16, MJ4=16, MJ5=16, CNB=32, MJB=16)
+_pack(F32, "KF", PM16=1, PM32=1, PM4=1, PMR=3, MH=3, CI=8, FA=8, FB=8, FC=8, FD0=8, FO=8, GO1=8, GO=8, NGO=8, RS=8, RV=8,
+      TAU=14, NTAU=14, PSC=14, PVC=14, R3=1, LA1=1, LA2=1, LAB=4, CT=4, IX=1, LD=8, PMH=1, BC=4)
+_pack(U16, "KU", FOU=8, RU=8, PU=28, NBU=24, CN=32, CIO=16, LN=16, NLD=32, FLD=16, LF=8, IDD=16, OFF8=8, PL=4, BO=8, JU=2, UO=32,
       LFIN=8)
-_sb(I32, NB=24, IOT=1024, KJ=512, FRI=128, SF=144, SFL=144, AB=136)
-_sb(F32, GR1=128, GR=128, JK=128, CMR=384, SAME=128, NEQ=128, SLT=128, KB=128, KAP=128, CMP=640, RLD=448, RLT=448,
-    PIO=128, NBR=384, D3=768, POS=1024, PT=512, FT=256, NP=128, UPD=1024, UG=256, LT=256, CK1=512, CK=512,
+_sb(I32, NB=24, IOT=1024, FRI=128, SF=144, SFL=144, AB=136, VL=256)
+_sb(F32, GR1=128, GR=128, JK=128, CMR=384, SAME=128, NEQ=128, SLT=128, KAP=128, CMP=640, RLD=448, RLT=448, LABT=1024, LBI=128,
+    PIO=128, NBR=384, D3=256, POS=1024, PT=512, FT=256, UGT=256, NP=128, UPD=2048, UG=256, LT=256, KJ=512, CKA=512, CKB=512, CK=512,
     NZ=128, RW=128, TR=128, SP=512, CM=512, JK4=512, MM=128, MT=128, GP=128, GPT=128, CC=128, T1=64, T2=64, T3=64,
     NDB=48, FPD=256, FPT=256, YS=128)
 _sb(U16, RQ=14, RQIN=14, GL0=2, GL1=2, RI0=8, RI1=8)
 _sb(B16, xb=512, bbb=512, ub=16, vb=16, ab=2048, wb=512, UT=512, VT=512, XT=512, BG=64)
-for _n, _w in (("XQ", 128), ("NW", 512), ("BBQ", 128), ("UQ", 128), ("VQ", 128), ("AQ", 512), ("WQ", 128), ("SL", 224), ("FW", 512),
+for _n, _w in (("XQ", 128), ("NW", 512), ("BBQ", 128), ("UQ", 128), ("VQ", 128), ("AQ", 512), ("WQ", 128), ("SL", 224), ("FW", 1280),
                ("PZ", 384), ("PX", 128), ("FIN", 128)):
     SCRATCH[_n] = ("sbuf", [128, _w], Q8)
     SCRATCH[_n + "S"] = ("sbuf", [128, _w], U8)
@@ -189,8 +189,11 @@ def rank_program(g, core, T, topo):
         emit("t", lambda: g.tensor.matmul_mx(ap(o), ap(a), ap(sc(a)), ap(b), ap(sc(b)), start, stop),
              [a, sc(a), b, sc(b)], [o])
 
-    def iota(o, pattern, cm=0):
-        emit("p", lambda: g.iota(ap(o), pattern, 0, cm), [], [o])
+    def iota(o, pattern, cm=0, base=0):
+        emit("p", lambda: g.iota(ap(o), pattern, base, cm), [], [o])
+
+    def fiota(o, pattern):
+        emit("p", lambda: g.iota(ap(o), pattern, 0, 0, allow_small_or_imprecise_dtypes=True), [], [o])
 
     peers = [(me + 1 + i) % n for i in range(n - 1)]
 
@@ -208,14 +211,18 @@ def rank_program(g, core, T, topo):
     def bits(m):
         return bin(m).count("1")
 
-    def each(srcs, dsts, sem, reads):
+    def each(plan, srcs, dsts, sem, reads):
         sync("p", reads, [])
-        trs = []
-        for i, s in enumerate(peers):
-            m = 1 << topo.engines(core, T.cores[s])[i]
-            trs.append(RemoteDMATransfer(dst_ids=[dst(s)], dma_engine_mask=m, remote_sem=T.sem[sem], src=srcs[i], dst=dsts[i]))
-        total["loc"] = total.get("loc", 0) + len(trs)
-        g.remote_dma_fused(trs, local_sem=T.sem.loc)
+        for call in plan:
+            trs = []
+            for i, es in call:
+                have = topo.engines(core, T.cores[peers[i]])
+                m = 0
+                for k in es:
+                    m |= 1 << have[k]
+                trs.append(RemoteDMATransfer(dst_ids=[dst(peers[i])], dma_engine_mask=m, remote_sem=T.sem[sem], src=srcs[i], dst=dsts[i]))
+                total["loc"] = total.get("loc", 0) + len(es)
+            g.remote_dma_fused(trs, local_sem=T.sem.loc)
 
     def spread(src, dsts, sem, reads):
         sync("p", reads, [])
@@ -223,6 +230,10 @@ def rank_program(g, core, T, topo):
         g.remote_dma_fused([RemoteDMATransfer(dst_ids=[dst(s) for s in peers], dma_engine_mask=shared, remote_sem=T.sem[sem],
                                               srcs=[src], dsts=dsts)], local_sem=T.sem.loc)
 
+    ONE = [[(i, [i]) for i in range(7)]]
+    FOUR = [(i, [2 * i, 2 * i + 1]) for i in range(4)]
+    CODES = [FOUR, [(4, [0, 1]), (5, [2, 3]), (6, [4, 5, 6, 7])]]
+    SCALES = [FOUR, [(4, [4, 5]), (5, [6, 7]), (6, [0, 1, 2, 3])]]
     u8 = dt.uint8
 
     for q, s, lo in (("y", "ln0", 0), ("s", "ln1", 4)):
@@ -230,8 +241,8 @@ def rank_program(g, core, T, topo):
             E[q].dma_start(T.NB[16 * k:16 * k + 16, :], T.nb[:]).then_inc(T.sem[s], 16)
         total[s] = 64
     recs["NB"] = [(X("NB"), "w", (s, 64, {s: 64}), "d") for s in ("ln0", "ln1")]
-    dma("y", "lx", [(T.xb[:], T.x[:])], [], [X("xb")])
     dma("s", "lu", [(T.ub[:], T.u[:, 0:16])], [], [X("ub")])
+    dma("y", "lx", [(T.xb[:], T.x[:])], [], [X("xb")])
     dma("s", "lv", [(T.vb[:], T.v[:, 0:16])], [], [X("vb")])
     dma("y", "lb", [(T.bbb[:], T.bb[:])], [], [X("bbb")])
     dma("y", "la", [(T.ab[:], T.a[:])], [], [X("ab")])
@@ -239,21 +250,31 @@ def rank_program(g, core, T, topo):
 
     iota(X("PID"), [[0, 1]], 1)
     iota(X("IOT"), [[1, 1024]])
+    fiota(X("KJ"), [[-32, 4], [1, 128]])
+    iota(X("CNB"), [[1, 2], [48, 8], [0, 2]])
+    iota(X("MJB"), [[48, 8], [0, 2]], 0, 2)
     iota(X("OFFC"), [[256, 4], [0, 2]])
-    iota(X("KJ"), [[-32, 4], [1, 128]])
-    emit("p", lambda: g.iota(ap(X("POS", 768, 1024)), [[64, 8], [0, 2], [4, 16]], 0, 0, allow_small_or_imprecise_dtypes=True),
-         [], [X("POS", 768, 1024)])
-    for m, k in (("PM16", 15), ("PM32", 31), ("PM4", 3)):
-        ts(X(m + "i"), X("PID"), k, OP.bitwise_and)
-        tc(X(m), X(m + "i"))
-    ts(X("W1"), X("PM16i"), 11, OP.mult)
-    ts(X("W2"), X("W1"), 5, OP.arith_shift_right)
-    ts(X("W3"), X("W2"), -3.0, OP.mult)
-    tt(X("RM3"), X("W3"), X("PM16"), OP.add)
-    for h in range(3):
-        ts(X("MH", h, h + 1), X("RM3"), float(2 - h), OP.is_equal)
+    fiota(X("POS", 768, 1024), [[64, 8], [0, 2], [4, 16]])
+    fiota(X("LABT"), [[32, 64], [1, 16]])
     fill(X("SF", 0, 8), -1)
     fill(X("SF", 8, 144), 0)
+    ts(X("PM16i"), X("PID"), 15, OP.bitwise_and)
+    ts(X("PM32i"), X("PID"), 31, OP.bitwise_and)
+    ts(X("PM4i"), X("PID"), 3, OP.bitwise_and)
+    ts(X("W1"), X("PM16i"), 11, OP.mult)
+    for h in range(3):
+        ts(X("PMR", h, h + 1), X("PM16i"), float(h - 2), OP.add)
+    ts(X("W2"), X("W1"), 5, OP.arith_shift_right)
+    tc(X("PM16"), X("PM16i"))
+    tc(X("PM4"), X("PM4i"))
+    tc(X("PM32"), X("PM32i"))
+    for h in range(3):
+        ts(X("MH", h, h + 1), X("W2"), 3.0, OP.mult, X("PMR", h, h + 1), OP.is_equal)
+    for i, c in enumerate((2.0 ** -25, 1.0, -1.0, float(-P * me))):
+        fill(X("BC", i, i + 1), c)
+    ts(X("UO"), X("IOT", 0, 32), 0.0, OP.mult, X("PM4"), OP.add)
+    ts(X("CI"), X("IOT", 0, 128, 16), X("PM16"), OP.add)
+    act(X("UT"), X("ub"), FN.Copy, off=X("UO"))
 
     for h, o in enumerate(("FA", "FB", "FC")):
         ts(X(o), X("NB", h, 24, 3), X("MH", h, h + 1), OP.mult)
@@ -261,7 +282,6 @@ def rank_program(g, core, T, topo):
     tt(X("FO"), X("FD0"), X("FC"), OP.add)
     tc(X("FOU"), X("FO"))
     gat(X("FRI"), X("IOT"), X("FOU"))
-    ts(X("CI"), X("IOT", 0, 128, 16), X("PM16"), OP.add)
     ts(X("GO1"), X("FO"), 128.0, OP.mult)
     ts(X("GR1"), X("FRI"), 128.0, OP.mult)
     tt(X("GO"), X("GO1"), X("CI"), OP.add)
@@ -275,21 +295,22 @@ def rank_program(g, core, T, topo):
     for t in range(NS, 8):
         red(X("RV", t, t + 1), X("CMR", 128 * (t - NS), 128 * (t - NS) + 128))
     tc(X("RU", NS, 8), X("RV", NS, 8))
+    act(X("VT"), X("vb"), FN.Copy, scale=-1.0, off=X("UO"))
     cut = 2 * (n - 1 - me)
-    if me < n - 1:
-        ts(X("TAU", 0, cut), X("IOT", SLOT * (me + 1), SLOT * n, 16), X("PM16"), OP.add)
-    if me > 0:
-        ts(X("TAU", cut, 14), X("IOT", 0, SLOT * me, 16), X("PM16"), OP.add)
+    for q in range(2):
+        if me < n - 1:
+            ts(X("TAU", q, cut, 2), X("IOT", P * (me + 1), P * n, P), X("PM16"), OP.add, 16.0 * q + 1, OP.add)
+        if me > 0:
+            ts(X("TAU", cut + q, 14, 2), X("IOT", 0, P * me, P), X("PM16"), OP.add, 16.0 * q + 1, OP.add)
     ts(X("NTAU"), X("TAU"), -1.0, OP.mult, 0.5, OP.add)
     ts(X("RU", 0, NS), X("RS", 0, NS), -0.5, OP.mult, 63.5, OP.add)
     sct(X("SF", 8, 136), X("RU"), X("FRI"))
     ts(X("AB", 7, 136), X("SF", 7, 136), 896, OP.bitwise_and)
     tt(X("NEQ"), X("SF", 8, 136), X("SF", 7, 135), OP.not_equal)
     tt(X("SAME"), X("AB", 8, 136), X("AB", 7, 135), OP.is_equal)
-    ts(X("KB"), X("AB", 8, 136), 0.25, OP.mult, -1.0, OP.add)
     emit("v", lambda: g.vector.tensor_tensor_scan(ap(X("SLT")), ap(X("SAME")), ap(X("NEQ")), 0.0, OP.mult, OP.add),
          [X("SAME"), X("NEQ")], [X("SLT")])
-    tt(X("KAP"), X("KB"), X("SLT"), OP.add)
+    tt(X("KAP"), X("AB", 8, 136), X("SLT"), OP.add)
     NT = 9
     for c in range(NT):
         act(X("JK"), X("KAP"), FN.Sign, bias=X("NTAU", c, c + 1), acc=X("PSC", c, c + 1))
@@ -305,74 +326,74 @@ def rank_program(g, core, T, topo):
     gat(X("RLD"), X("SFL", 8, 144), X("PU"))
     tr(X("RLT"), X("RLD"))
     tc(X("RQ"), X("RLT", 0, 448, 32))
-    each([T.RQ[:, 2 * i:2 * i + 2] for i in range(n - 1)],
+    each(ONE, [T.RQ[:, 2 * i:2 * i + 2] for i in range(n - 1)],
          [T.RQIN[:, 2 * slot_at(s):2 * slot_at(s) + 2] for s in peers], "rq", [X("RQ")])
 
     quant(X("XQ"), X("xb"))
-    quant(X("NW", 0, 128), X("xb"))
-    ts(X("UO"), X("IOT", 0, 32), 0.0, OP.mult, X("PM4"), OP.add)
-    act(X("UT"), X("ub"), FN.Copy, off=X("UO"))
-    act(X("VT"), X("vb"), FN.Copy, scale=-1.0, off=X("UO"))
     tc(X("NBU"), X("NB"))
     gat(X("NBR"), X("IOT"), X("NBU"))
     ts(X("R3"), X("PM16"), 3.0, OP.mult)
-    for k in range(3):
-        for d in range(2):
-            ts(X("CN", 16 * k + d, 16 * k + 16, 2), X("IOT", k, 384, 48), X("R3"), OP.add)
-    act(X("D3"), X("NBR"), FN.Copy, off=X("CN"))
+    ts(X("CN"), X("CNB"), X("R3"), OP.add)
+    act(X("LBI"), X("LABT"), FN.Copy, off=X("FOU"))
+    act(X("POS", 0, 512), X("NBR"), FN.Identity, bias=X("BC", 3, 4), off=X("CN"))
+    ts(X("MJ"), X("MJB"), X("R3"), OP.add)
+    quant(X("NW", 0, 128), X("xb"))
+    ts(X("MJ2"), X("MJ"), 4, OP.arith_shift_right)
     quant(X("UQ"), X("UT"))
+    ts(X("MJ3"), X("MJ2"), 171, OP.mult)
     quant(X("VQ"), X("VT"))
-    quant(X("BBQ"), X("bbb"))
+    ts(X("MJ4"), X("MJ3"), 9, OP.arith_shift_right)
+    ts(X("MJ2"), X("MJ"), 15, OP.bitwise_and)
+    ts(X("MJ5"), X("MJ4"), 16, OP.mult)
+    tt(X("MJ3"), X("MJ2"), X("MJ5"), OP.add)
+    tc(X("CIO"), X("MJ3"))
 
     arrive("rq", n - 1, [X("RQIN")])
     pick(X("SL"), X("XQ"), X("RQIN"))
-    blocks = [(SLOT * i, SLOT * i + LC) for i in range(n - 1)]
-    land = (SLOT * me, SLOT * me + LC)
-    each([T.SL[:, a:b].bitcast(u8) for a, b in blocks], [T.FW[:, land[0]:land[1]].bitcast(u8) for s in peers], "rc", [X("SL")])
-    each([T.SLS[:, a:b] for a, b in blocks], [T.FWS[:, land[0]:land[1]] for s in peers], "rs", [X("SLS")])
-    arrive("rc", n - 1, [X("FW", 0, 256)])
-    arrive("rs", n - 1, [X("FWS", 0, 256)])
-
-    ts(X("POS", 0, 512), X("D3", 0, 512), float(-P * me), OP.add)
-    tr(X("PT"), X("POS", 0, 512))
-    tc(X("LN"), X("PT", 0, 512, 32))
+    blocks = [(32 * i, 32 * i + LC) for i in range(n - 1)]
+    land = (P * me, P * me + LC)
+    each(CODES, [T.SL[:, a:b].bitcast(u8) for a, b in blocks], [T.FW[:, land[0]:land[1]].bitcast(u8) for s in peers], "rc", [X("SL")])
+    each(SCALES, [T.SLS[:, a:b] for a, b in blocks], [T.FWS[:, land[0]:land[1]] for s in peers], "rs", [X("SLS")])
+    for s, w in (("rc", "FW"), ("rs", "FWS")):
+        arrive(s, sum(len(es) for call in CODES for i, es in call), [X(w, 0, 1024)])
+    iota(X("VL"), [[1, 256]], 0, 1024)
+    fiota(X("UPD"), [[0, 2048]])
 
     def near_sums():
         pick(X("PZ", 0, 256), X("NW"), X("LN"))
         mm("Z", X("UQ"), X("PZ", 0, 128), True, False)
         mm("Z", X("UQ"), X("PZ", 128, 256), False, False)
+    act(X("PIO"), X("KAP"), FN.Copy, off=X("RU"))
+    act(X("POS", 512, 768), X("PIO"), FN.Identity, bias=X("BC", 2, 3), off=X("CIO"))
+    tr(X("PT"), X("POS", 0, 512))
+    tc(X("LN"), X("PT", 0, 512, 32))
     near_sums()
-    ts(X("MJ"), X("IOT", 2, 384, 48), X("R3"), OP.add)
-    ts(X("MJ2"), X("MJ"), 4, OP.arith_shift_right)
-    ts(X("MJ3"), X("MJ2"), 171, OP.mult)
-    ts(X("MJ4"), X("MJ3"), 9, OP.arith_shift_right)
-    ts(X("MJ2"), X("MJ"), 15, OP.bitwise_and)
-    ts(X("MJ3"), X("MJ4"), 16, OP.mult)
-    for d in range(2):
-        tt(X("LT", 8 * d, 8 * d + 8), X("MJ2"), X("MJ3"), OP.add)
-        tc(X("CIO", d, 16, 2), X("LT", 8 * d, 8 * d + 8))
-    gat(X("PIO"), X("KAP"), X("RU"))
-    gat(X("POS", 512, 768), X("PIO"), X("CIO"))
     tr(X("FT"), X("POS", 512, 768))
     tc(X("LF"), X("FT", 0, 256, 32))
-    ts(X("CK1"), X("KJ"), X("PM32"), OP.is_lt, -2.0 ** -24, OP.mult)
-    ts(X("CK"), X("CK1"), 1.0, OP.add)
+    quant(X("BBQ"), X("bbb"))
+    ts(X("PMH"), X("PM32"), -0.5, OP.add)
+    act(X("CKA"), X("KJ"), FN.Sign, bias=X("PMH"), scale=-1.0)
+    act(X("CKB"), X("CKA"), FN.Identity, bias=X("BC", 0, 1), scale=2.0 ** -25)
+    act(X("CK"), X("CKB"), FN.Identity, bias=X("BC", 1, 2), scale=-1.0)
     ts(X("LA1"), X("PM32"), 16.0, OP.is_ge, 16.0, OP.mult)
-    tt(X("LA2"), X("LA1"), X("PM32"), OP.add)
-    ts(X("LAB"), X("IOT", 0, 256, 64), X("LA2"), OP.add)
     ts(X("IO16"), X("IOT", 0, 32), 15, OP.bitwise_and)
+    tt(X("LA2"), X("LA1"), X("PM32"), OP.add)
     for b in range(4):
         quant(X("AQ", 128 * b, 128 * b + 128), X("ab", 512 * b, 512 * b + 512))
+    ts(X("LAB"), X("IOT", 0, 256, 64), X("LA2"), OP.add)
     quant(X("PX"), X("xb"))
     fill(X("XT"), 0.0)
+    tc(X("NP"), X("IOT", 0, 128))
 
     c05 = float(np.float32(0.05))
     TINY = 2.0 ** -100
     for t in range(R):
-        fw = (256, 384, 512)[t]
+        fw = (1024, 1152, 1280)[t]
         pick(X("PZ", 256, 384), X("FW", 0, fw), X("LF"))
         mm("Z", X("UQ"), X("PZ", 256, 384), False, False)
         mm("Z", X("VQ"), X("BBQ"), False, True)
+        if t:
+            tt(X("POS", 512, 768), X("POS", 512, 768), X("UG"), OP.max)
         z = X("Z", 0, 128)
         ts(X("NZ"), z, -1.0, OP.mult, TINY, OP.max)
         tt(X("RW"), z, X("NZ"), OP.max)
@@ -388,29 +409,26 @@ def rank_program(g, core, T, topo):
         tr(X("MT"), X("MM"))
         red(X("IX"), X("MT"))
         ts(X("OFF8"), X("OFFC"), X("IX"), OP.add)
+        if t < R - 1:
+            gl = "GL%d" % t
+            ts(X(gl, 0, 1), X("IX"), 256.0 * me, OP.add)
+            spread(T[gl][:, 0:1], [T["RI%d" % t][:, slot_at(s):slot_at(s) + 1] for s in peers], "li%d" % t, [X(gl, 0, 1)])
         gat(X("GP"), X("POS"), X("OFF8"))
         tr(X("GPT"), X("GP"))
         tc(X("PL"), X("GPT", 0, 128, 32))
+        j4 = X("GPT", 96, 97)
         pick(X("PX", 0, 32), X("NW", 0, 128 * (t + 1)), X("PL", 0, 2))
         pick(X("PX", 32, 48), X("FW", 0, fw), X("PL", 2, 3))
         for b in range(4):
             mm("S%d" % b, X("AQ", 128 * b, 128 * b + 128), X("PX"))
-        j4 = X("GPT", 96, 97)
-        gl = "GL%d" % t
-        if t < R - 1:
-            ts(X(gl, 0, 1), j4, 0.25, OP.mult, float(P * me), OP.add)
-            spread(T[gl][:, 0:1], [T["RI%d" % t][:, slot_at(s):slot_at(s) + 1] for s in peers], "li%d" % t, [X(gl, 0, 1)])
         ts(X("BO", 0, 8, 2), X("IOT", 0, 4), j4, OP.add)
         ts(X("JU", 0, 1), j4, 0.25, OP.mult)
         for b in range(4):
             act(X("BG", b, 64, 4), X("bbb"), FN.Copy, off=X("BO", 2 * b, 2 * b + 1))
+        sct(X("NP"), X("JU", 0, 1), X("IOT", P * (t + 1), P * (t + 1) + K))
         if t == 0:
-            tc(X("NP"), X("IOT", 0, 128))
-
-        def moved():
-            sct(X("NP"), X("JU", 0, 1), X("IOT", P * (t + 1), P * (t + 1) + K))
+            tc(X("NLD"), X("PT", 0, 512, 16))
         if t == R - 1:
-            moved()
             for d in range(2):
                 tc(X("IDD", d, 16, 2), X("CI"))
             gat(X("FPD"), X("NP"), X("IDD"))
@@ -419,6 +437,8 @@ def rank_program(g, core, T, topo):
         for b in range(4):
             act(X("CC", 32 * b, 32 * b + 32), X("S%d" % b, 16, 48), FN.Copy)
             tt(X("T1", b, 64, 4), X("S%d" % b, 0, 16), X("CC", 32 * b, 32 * b + 16), OP.add)
+        if t < R - 1:
+            act(X("POS", 0, 512), X("NP"), FN.Copy, off=X("NLD"))
         for b in range(4):
             tt(X("T2", b, 64, 4), X("T1", b, 64, 4), X("CC", 32 * b + 16, 32 * b + 32), OP.add)
         ts(X("T3"), X("T2"), c05, OP.mult)
@@ -430,26 +450,22 @@ def rank_program(g, core, T, topo):
                    [T.FW[:, fw + K * slot_at(s):fw + K * slot_at(s) + K].bitcast(u8) for s in peers], "cd%d" % t, [X("NW", new, new + K)])
             spread(T.NWS[:, new:new + K],
                    [T.FWS[:, fw + K * slot_at(s):fw + K * slot_at(s) + K] for s in peers], "sc%d" % t, [X("NWS", new, new + K)])
-            emit("v", lambda: g.vector.tensor_scalar(T.NDB[0:1, K * t:K * t + K], T.GP[0:1, 96:112], 0.25, None, OP.mult),
-                 [X("GP")], [X("NDB", K * t, K * t + K)])
-            moved()
             if t == 0:
-                for d in range(2):
-                    tc(X("NLD", d, 32, 2), X("LN"))
-                tr(X("LT"), X("D3", 512, 768))
-                for d in range(2):
-                    tc(X("FLD", d, 16, 2), X("LT", 0, 256, 32))
-                fill(X("UPD"), 0.0)
-            gat(X("POS", 0, 512), X("NP"), X("NLD"))
+                act(X("D3"), X("LBI"), FN.Copy, off=X("CIO"))
             tr(X("PT"), X("POS", 0, 512))
             tc(X("LN"), X("PT", 0, 512, 32))
             near_sums()
+            if t == 0:
+                tr(X("LT"), X("D3"))
+                tc(X("FLD"), X("LT", 0, 256, 16))
             arrive("li%d" % t, (n - 1) * bits(shared), [X("RI%d" % t, 0, 7)])
-            sct(X("UPD"), X("RI%d" % t, 0, 7), X("IOT", fw, fw + 112))
+            sct(X("UPD"), X("RI%d" % t, 0, 7), X("VL", fw - 1024, fw - 1024 + 112))
             gat(X("UG"), X("UPD"), X("FLD"))
-            tt(X("POS", 512, 768), X("POS", 512, 768), X("UG"), OP.max)
-            tr(X("FT"), X("POS", 512, 768))
-            tc(X("LF"), X("FT", 0, 256, 32))
+            tr(X("UGT"), X("UG"))
+            tt(X("LD"), X("FT", 0, 256, 32), X("UGT", 0, 256, 32), OP.max)
+            tc(X("LF"), X("LD"))
+            emit("v", lambda: g.vector.tensor_scalar(T.NDB[0:1, K * t:K * t + K], T.GP[0:1, 96:112], 0.25, None, OP.mult),
+                 [X("GP")], [X("NDB", K * t, K * t + K)])
             if t == 0:
                 quant(X("WQ"), X("wb"))
             arrive("cd%d" % t, (n - 1) * bits(shared), [X("FW", fw, fw + 112)])

@@ -21,26 +21,29 @@ def _pack(kind, big, **names):
     SCRATCH[big] = ("sbuf", [128, at], kind)
 
 
-_pack(I32, "KI", PID=1, PM16i=1, PM32i=1, PM4i=1, W1=1, W2=1, IO16=32, OFFC=8, MJ=16, MJ2=16, MJ3=16, MJ4=16, MJ5=16, CNB=32, MJB=16)
-_pack(F32, "KF", PM16=1, PM32=1, PM4=1, PMR=3, MH=3, CI=8, FA=8, FB=8, FC=8, FD0=8, FO=8, GO1=8, GO=8, NGO=8, RS=8, RV=8,
-      TAU=14, NTAU=14, PSC=14, PVC=14, R3=1, LA1=1, LA2=1, LAB=4, CT=4, IX=1, LD=8, PMH=1, BC=4)
-_pack(U16, "KU", FOU=8, RU=8, PU=28, NBU=24, CN=32, CIO=16, LN=16, NLD=32, FLD=16, LF=8, IDD=16, OFF8=8, PL=4, BO=8, JU=2, UO=32,
-      LFIN=8)
-_sb(I32, NB=24, IOT=1024, FRI=128, SF=144, SFL=144, AB=136, VL=256)
-_sb(F32, GR1=128, GR=128, JK=128, CMR=384, SAME=128, NEQ=128, SLT=128, KAP=128, CMP=640, RLD=448, RLT=448, LABT=1024, LBI=128,
-    PIO=128, NBR=384, D3=256, POS=1024, PT=512, FT=256, UGT=256, NP=128, UPD=2048, UG=256, LT=256, KJ=512, CKA=512, CKB=512, CK=512,
-    NZ=128, RW=128, TR=128, SP=512, CM=512, JK4=512, MM=128, MT=128, GP=128, GPT=128, CC=128, T1=64, T2=64, T3=64,
+_pack(I32, "KI", PID=1, PM16i=1, PM32i=1, W1=1, W2=1, II=32, IO16=32, MJ=16, MJ2=16, MJ3=16, MJ4=16, MJ5=16, CNB=32, MJB=16)
+_pack(F32, "KF", PM16=1, PM32=1, PMR=3, MH=3, CI=8, CI128=8, NCI=8, FA=8, FB=8, FC=8, FD0=8, FO=8, GO=8, NGO=8, RS=8, RV=8,
+      G8=1, TSH=3, NTAU=8, NPM=1, BASE=8, PC=11, PVC=8, R3=1, LA1=1, LA2=1, LAB=4, CT=4, IX=1, LD=8, PMH=1, BC=4, NVC=4, OFFC=8,
+      KJ=32, CKA=32, CKB=32, CK=32, OXF=64, VAL=32)
+_pack(U16, "KU", FOU=8, RU=8, PU=24, NBU=24, CN=32, CIO=16, LN=16, NLD=32, FLD=16, LF=8, IDD=16, OFF8=8, PL=4, BO=8, JU=2, OX=64,
+      LFIN=8, JL=2)
+_sb(I32, NB=24, SF=144, SFL=144, AB=136, VL=256)
+_sb(F32, JT=1024, PLK=128, FRF=128, GR=128, JKA=768, JKB=896, CMR=256, NEQ=128, ABF=128, KAP=128, CMP=512, RLD=352, RLT=352, LABT=1024,
+    LBI=128, PIO=128, NBR=384, D3=256, POS=1024, PT=512, FT=256, UGT=256, NP=128, UPD=2048, UG=256, LT=256,
+    ETR=128, EXP=1024, ETAB=1024, E3=384, E01=128, E2=128, ZS=128,
+    NZ=128, RW=128, TR=128, SP=128, CM=512, JK4=512, MM=128, MT=128, GP=128, GPT=128, CC=128, T1=64, T2=64, T3=64,
     NDB=48, FPD=256, FPT=256, YS=128)
-_sb(U16, RQ=14, RQIN=14, GL0=2, GL1=2, RI0=8, RI1=8)
+_sb(F32, ET=32)
+_sb(U16, RQ=12, RQIN=14, GL0=2, GL1=2, RI0=8, RI1=8)
 _sb(B16, xb=512, bbb=512, ub=16, vb=16, ab=2048, wb=512, UT=512, VT=512, XT=512, BG=64)
 for _n, _w in (("XQ", 128), ("NW", 512), ("BBQ", 128), ("UQ", 128), ("VQ", 128), ("AQ", 512), ("WQ", 128), ("SL", 224), ("FW", 1280),
-               ("PZ", 384), ("PX", 128), ("FIN", 128)):
+               ("PZ", 384), ("PX", 256), ("FIN", 128)):
     SCRATCH[_n] = ("sbuf", [128, _w], Q8)
     SCRATCH[_n + "S"] = ("sbuf", [128, _w], U8)
-BANKS = ("Z", "S0", "S1", "S2", "S3", "Y")
+BANKS = ("Z", "S0", "S1", "S2", "S3", "Y", "EB", "FB0")
 for _n in BANKS:
     SCRATCH[_n] = ("psum", [128, 512], F32)
-SEMAPHORES = ["cv", "cs", "ct", "cp", "ln0", "ln1", "lx", "lb", "lu", "lv", "la", "lw", "rq", "rc", "rs", "loc",
+SEMAPHORES = ["cv", "cs", "ct", "cp", "ln0", "ln1", "lx", "lb", "lu", "lv", "la", "lw", "ee", "rq", "rc", "rs", "loc",
               "li0", "li1", "cd0", "cd1", "sc0", "sc1", "on", "oc", "os", "oy"]
 
 
@@ -192,8 +195,8 @@ def rank_program(g, core, T, topo):
     def iota(o, pattern, cm=0, base=0):
         emit("p", lambda: g.iota(ap(o), pattern, base, cm), [], [o])
 
-    def fiota(o, pattern):
-        emit("p", lambda: g.iota(ap(o), pattern, 0, 0, allow_small_or_imprecise_dtypes=True), [], [o])
+    def fiota(o, pattern, base=0):
+        emit("p", lambda: g.iota(ap(o), pattern, base, 0, allow_small_or_imprecise_dtypes=True), [], [o])
 
     peers = [(me + 1 + i) % n for i in range(n - 1)]
 
@@ -249,161 +252,204 @@ def rank_program(g, core, T, topo):
     dma("y", "lw", [(T.wb[:], T.w[:])], [], [X("wb")])
 
     iota(X("PID"), [[0, 1]], 1)
-    iota(X("IOT"), [[1, 1024]])
-    fiota(X("KJ"), [[-32, 4], [1, 128]])
+    fiota(X("JT", 0, 256), [[1, 256]])
+    iota(X("II"), [[1, 32]])
+    fiota(X("OXF"), [[1, 32], [0, 2]])
+    wrap = n - 1 - me
+    for lo, hi, base in ((0, wrap, -P * (me + 1)), (wrap, 8, 0)):
+        if lo < hi and lo % 2:
+            fiota(X("BASE", lo, lo + 1), [[0, 1]], base - 8)
+            lo, base = lo + 1, base - P
+        if hi - lo > 1:
+            fiota(X("BASE", lo, hi - hi % 2), [[-2 * P, (hi - lo) // 2], [-P - 8, 2]], base)
+        if hi % 2 and lo < hi:
+            fiota(X("BASE", hi - 1, hi), [[0, 1]], base - P * (hi - 1 - lo))
     iota(X("CNB"), [[1, 2], [48, 8], [0, 2]])
     iota(X("MJB"), [[48, 8], [0, 2]], 0, 2)
-    iota(X("OFFC"), [[256, 4], [0, 2]])
-    fiota(X("POS", 768, 1024), [[64, 8], [0, 2], [4, 16]])
-    fiota(X("LABT"), [[32, 64], [1, 16]])
+    fiota(X("OFFC"), [[256, 4], [0, 2]])
+    fiota(X("KJ"), [[1, 32]])
     fill(X("SF", 0, 8), -1)
     fill(X("SF", 8, 144), 0)
     ts(X("PM16i"), X("PID"), 15, OP.bitwise_and)
     ts(X("PM32i"), X("PID"), 31, OP.bitwise_and)
-    ts(X("PM4i"), X("PID"), 3, OP.bitwise_and)
     ts(X("W1"), X("PM16i"), 11, OP.mult)
+    tc(X("PM16"), X("PM16i"))
     for h in range(3):
         ts(X("PMR", h, h + 1), X("PM16i"), float(h - 2), OP.add)
     ts(X("W2"), X("W1"), 5, OP.arith_shift_right)
-    tc(X("PM16"), X("PM16i"))
-    tc(X("PM4"), X("PM4i"))
-    tc(X("PM32"), X("PM32i"))
+    ts(X("G8"), X("PM16"), 7.5, OP.is_gt)
     for h in range(3):
         ts(X("MH", h, h + 1), X("W2"), 3.0, OP.mult, X("PMR", h, h + 1), OP.is_equal)
-    for i, c in enumerate((2.0 ** -25, 1.0, -1.0, float(-P * me))):
-        fill(X("BC", i, i + 1), c)
-    ts(X("UO"), X("IOT", 0, 32), 0.0, OP.mult, X("PM4"), OP.add)
-    ts(X("CI"), X("IOT", 0, 128, 16), X("PM16"), OP.add)
-    act(X("UT"), X("ub"), FN.Copy, off=X("UO"))
+    ts(X("JT", 256, 512), X("JT", 0, 256), 256.0, OP.add)
+    ts(X("CI"), X("JT", 0, 128, 16), X("PM16"), OP.add)
+    ts(X("PLK"), X("JT", 0, 128), 1.0 / P, OP.mult)
+    ts(X("CI128"), X("CI"), 1.0 / P, OP.mult)
+    ts(X("NCI"), X("CI"), -1.0 / P, OP.mult)
+    ts(X("JT", 512, 1024), X("JT", 0, 512), 512.0, OP.add)
+    for b in range(4):
+        act(X("UT", b, 512, 4), X("JT", 0, 128), FN.Identity, bias=X("ub", b, b + 1), scale=0.0)
+
+    def shared_column(m):
+        ts(X("TSH", m, m + 1), X("G8"), float(P * (peers[2 * m + 1] - peers[2 * m]) - LC), OP.mult, X("PM16"), OP.add)
 
     for h, o in enumerate(("FA", "FB", "FC")):
         ts(X(o), X("NB", h, 24, 3), X("MH", h, h + 1), OP.mult)
     tt(X("FD0"), X("FA"), X("FB"), OP.add)
+    shared_column(0)
     tt(X("FO"), X("FD0"), X("FC"), OP.add)
+    shared_column(1)
     tc(X("FOU"), X("FO"))
-    gat(X("FRI"), X("IOT"), X("FOU"))
-    ts(X("GO1"), X("FO"), 128.0, OP.mult)
-    ts(X("GR1"), X("FRI"), 128.0, OP.mult)
-    tt(X("GO"), X("GO1"), X("CI"), OP.add)
-    tt(X("GR"), X("GR1"), X("IOT", 0, 128), OP.add)
-    ts(X("NGO"), X("GO"), -1.0, OP.mult)
-    NS = 5
+    tt(X("GO"), X("FO"), X("CI128"), OP.add)
+    tt(X("NGO"), X("NCI"), X("FO"), OP.subtract)
+    emit("v", lambda: g.vector.tensor_tensor(ap(X("GR")), ap(X("JT")).indirect(ap(X("FOU"))), ap(X("PLK")), OP.add),
+         [X("JT"), X("FOU"), X("PLK")], [X("GR")])
+    act(X("FRF"), X("JT"), FN.Copy, off=X("FOU"))
+    NS = 6
     for t in range(NS):
-        act(X("JK"), X("GR"), FN.Sign, bias=X("NGO", t, t + 1), acc=X("RS", t, t + 1))
+        act(X("JKA", 128 * t, 128 * t + 128), X("GR"), FN.Sign, bias=X("NGO", t, t + 1), acc=X("RS", t, t + 1))
+    quant(X("XQ"), X("xb"))
+    quant(X("UQ"), X("UT"))
+    mm("EB", X("UQ"), X("XQ"))
     for t in range(NS, 8):
         ts(X("CMR", 128 * (t - NS), 128 * (t - NS) + 128), X("GR"), X("GO", t, t + 1), OP.is_lt)
+    tr(X("ETR"), X("EB", 0, 128))
     for t in range(NS, 8):
         red(X("RV", t, t + 1), X("CMR", 128 * (t - NS), 128 * (t - NS) + 128))
+    own = X("ET", 4 * me, 4 * me + 4)
+    tc(own, X("ETR", 0, 128, 32))
+    spread(ap(own), [ap(own) for s in peers], "ee", [own])
+    for lo, hi in ((0, 4 * me), (4 * me + 4, 32)):
+        if lo < hi:
+            arrive("ee", (n - 1) * bits(shared), [X("ET", lo, hi)])
+    fiota(X("LABT"), [[32, 64], [1, 16]])
+    fiota(X("POS", 768, 1024), [[64, 8], [0, 2], [4, 16]])
     tc(X("RU", NS, 8), X("RV", NS, 8))
-    act(X("VT"), X("vb"), FN.Copy, scale=-1.0, off=X("UO"))
-    cut = 2 * (n - 1 - me)
-    for q in range(2):
-        if me < n - 1:
-            ts(X("TAU", q, cut, 2), X("IOT", P * (me + 1), P * n, P), X("PM16"), OP.add, 16.0 * q + 1, OP.add)
-        if me > 0:
-            ts(X("TAU", cut + q, 14, 2), X("IOT", 0, P * me, P), X("PM16"), OP.add, 16.0 * q + 1, OP.add)
-    ts(X("NTAU"), X("TAU"), -1.0, OP.mult, 0.5, OP.add)
     ts(X("RU", 0, NS), X("RS", 0, NS), -0.5, OP.mult, 63.5, OP.add)
-    sct(X("SF", 8, 136), X("RU"), X("FRI"))
-    ts(X("AB", 7, 136), X("SF", 7, 136), 896, OP.bitwise_and)
+    ts(X("NPM"), X("PM16"), -1.0, OP.mult, 0.5, OP.add)
+    sct(X("SF", 8, 136), X("RU"), X("FRF"))
+    ts(X("NTAU"), X("BASE"), X("NPM"), OP.add)
+    ts(X("AB"), X("SF", 8, 144), 896, OP.bitwise_and)
     tt(X("NEQ"), X("SF", 8, 136), X("SF", 7, 135), OP.not_equal)
-    tt(X("SAME"), X("AB", 8, 136), X("AB", 7, 135), OP.is_equal)
-    emit("v", lambda: g.vector.tensor_tensor_scan(ap(X("SLT")), ap(X("SAME")), ap(X("NEQ")), 0.0, OP.mult, OP.add),
-         [X("SAME"), X("NEQ")], [X("SLT")])
-    tt(X("KAP"), X("AB", 8, 136), X("SLT"), OP.add)
-    NT = 9
-    for c in range(NT):
-        act(X("JK"), X("KAP"), FN.Sign, bias=X("NTAU", c, c + 1), acc=X("PSC", c, c + 1))
-    for c in range(NT, 14):
-        ts(X("CMP", 128 * (c - NT), 128 * (c - NT) + 128), X("KAP"), X("TAU", c, c + 1), OP.is_lt)
-    for c in range(NT, 14):
-        red(X("PVC", c, c + 1), X("CMP", 128 * (c - NT), 128 * (c - NT) + 128))
+    tc(X("ABF"), X("AB", 0, 128))
+    shared_column(2)
+    emit("v", lambda: g.vector.tensor_tensor_scan(ap(X("KAP")), ap(X("NEQ")), ap(X("ABF")), -1.0, OP.add, OP.max),
+         [X("NEQ"), X("ABF")], [X("KAP")])
+    for i in range(n - 1):
+        c = 3 * (i // 2) + 2 * (i % 2)
+        act(X("JKB", 128 * i, 128 * i + 128), X("KAP"), FN.Sign, bias=X("NTAU", i, i + 1), acc=X("PC", c, c + 1))
+    for m in range(4):
+        than = X("TSH", m, m + 1) if m < 3 else X("PM16")
+        ts(X("CMP", 128 * m, 128 * m + 128), X("KAP"), P * peers[2 * m] + 16.0, OP.subtract, than, OP.is_lt)
+    for m in range(4):
+        red(X("PVC", m, m + 1), X("CMP", 128 * m, 128 * m + 128))
     ts(X("SFL", 8, 144), X("SF", 8, 144), 127, OP.bitwise_and)
+    ts(X("PC", 1, 11, 3), X("PVC", 0, 4), -2.0, OP.mult, float(P), OP.add)
     for d in range(2):
-        tc(X("PU", 2 * NT + d, 28, 2), X("PVC", NT, 14))
-    for d in range(2):
-        ts(X("PU", d, 2 * NT, 2), X("PSC", 0, NT), -0.5, OP.mult, 64.0, OP.add)
-    gat(X("RLD"), X("SFL", 8, 144), X("PU"))
+        ts(X("PU", d, 22, 2), X("PC"), -0.5, OP.mult, 64.0, OP.add)
+    gat(X("RLD"), X("SFL", 8, 144), X("PU", 0, 22))
     tr(X("RLT"), X("RLD"))
-    tc(X("RQ"), X("RLT", 0, 448, 32))
-    each(ONE, [T.RQ[:, 2 * i:2 * i + 2] for i in range(n - 1)],
+    tc(X("RQ", 0, 11), X("RLT", 0, 352, 32))
+    first = [3 * (i // 2) + i % 2 for i in range(n - 1)]
+    each(ONE, [T.RQ[:, c:c + 2] for c in first],
          [T.RQIN[:, 2 * slot_at(s):2 * slot_at(s) + 2] for s in peers], "rq", [X("RQ")])
+    fiota(X("UPD"), [[0, 2048]])
+    iota(X("VL"), [[1, 256]], 0, 1024)
 
-    quant(X("XQ"), X("xb"))
     tc(X("NBU"), X("NB"))
-    gat(X("NBR"), X("IOT"), X("NBU"))
+    tc(X("OX"), X("OXF"))
     ts(X("R3"), X("PM16"), 3.0, OP.mult)
+    for i, c in enumerate((2.0 ** -25, 1.0, float(-P * me))):
+        fill(X("BC", i, i + 1), c)
     ts(X("CN"), X("CNB"), X("R3"), OP.add)
-    act(X("LBI"), X("LABT"), FN.Copy, off=X("FOU"))
-    act(X("POS", 0, 512), X("NBR"), FN.Identity, bias=X("BC", 3, 4), off=X("CN"))
+    ts(X("NVC"), X("vb", 0, 4), -1.0, OP.mult)
+    for b in range(4):
+        act(X("VT", b, 512, 4), X("JT", 0, 128), FN.Identity, bias=X("NVC", b, b + 1), scale=0.0)
+    gat(X("NBR"), X("JT"), X("NBU"))
+    act(X("POS", 0, 512), X("NBR"), FN.Identity, bias=X("BC", 2, 3), off=X("CN"))
     ts(X("MJ"), X("MJB"), X("R3"), OP.add)
     quant(X("NW", 0, 128), X("xb"))
     ts(X("MJ2"), X("MJ"), 4, OP.arith_shift_right)
-    quant(X("UQ"), X("UT"))
-    ts(X("MJ3"), X("MJ2"), 171, OP.mult)
     quant(X("VQ"), X("VT"))
+    ts(X("MJ3"), X("MJ2"), 171, OP.mult)
+    quant(X("BBQ"), X("bbb"))
+    mm("FB0", X("VQ"), X("BBQ"))
     ts(X("MJ4"), X("MJ3"), 9, OP.arith_shift_right)
     ts(X("MJ2"), X("MJ"), 15, OP.bitwise_and)
     ts(X("MJ5"), X("MJ4"), 16, OP.mult)
     tt(X("MJ3"), X("MJ2"), X("MJ5"), OP.add)
     tc(X("CIO"), X("MJ3"))
-
-    arrive("rq", n - 1, [X("RQIN")])
-    pick(X("SL"), X("XQ"), X("RQIN"))
-    blocks = [(32 * i, 32 * i + LC) for i in range(n - 1)]
-    land = (P * me, P * me + LC)
-    each(CODES, [T.SL[:, a:b].bitcast(u8) for a, b in blocks], [T.FW[:, land[0]:land[1]].bitcast(u8) for s in peers], "rc", [X("SL")])
-    each(SCALES, [T.SLS[:, a:b] for a, b in blocks], [T.FWS[:, land[0]:land[1]] for s in peers], "rs", [X("SLS")])
-    for s, w in (("rc", "FW"), ("rs", "FWS")):
-        arrive(s, sum(len(es) for call in CODES for i, es in call), [X(w, 0, 1024)])
-    iota(X("VL"), [[1, 256]], 0, 1024)
-    fiota(X("UPD"), [[0, 2048]])
-
-    def near_sums():
-        pick(X("PZ", 0, 256), X("NW"), X("LN"))
-        mm("Z", X("UQ"), X("PZ", 0, 128), True, False)
-        mm("Z", X("UQ"), X("PZ", 128, 256), False, False)
     act(X("PIO"), X("KAP"), FN.Copy, off=X("RU"))
-    act(X("POS", 512, 768), X("PIO"), FN.Identity, bias=X("BC", 2, 3), off=X("CIO"))
-    tr(X("PT"), X("POS", 0, 512))
-    tc(X("LN"), X("PT", 0, 512, 32))
-    near_sums()
-    tr(X("FT"), X("POS", 512, 768))
-    tc(X("LF"), X("FT", 0, 256, 32))
-    quant(X("BBQ"), X("bbb"))
+    act(X("POS", 512, 768), X("PIO"), FN.Copy, off=X("CIO"))
+    tc(X("PM32"), X("PM32i"))
     ts(X("PMH"), X("PM32"), -0.5, OP.add)
     act(X("CKA"), X("KJ"), FN.Sign, bias=X("PMH"), scale=-1.0)
     act(X("CKB"), X("CKA"), FN.Identity, bias=X("BC", 0, 1), scale=2.0 ** -25)
     act(X("CK"), X("CKB"), FN.Identity, bias=X("BC", 1, 2), scale=-1.0)
     ts(X("LA1"), X("PM32"), 16.0, OP.is_ge, 16.0, OP.mult)
-    ts(X("IO16"), X("IOT", 0, 32), 15, OP.bitwise_and)
+    ts(X("IO16"), X("II"), 15, OP.bitwise_and)
     tt(X("LA2"), X("LA1"), X("PM32"), OP.add)
     for b in range(4):
         quant(X("AQ", 128 * b, 128 * b + 128), X("ab", 512 * b, 512 * b + 512))
-    ts(X("LAB"), X("IOT", 0, 256, 64), X("LA2"), OP.add)
-    quant(X("PX"), X("xb"))
+    ts(X("LAB"), X("JT", 0, 256, 64), X("LA2"), OP.add)
+    for b in range(2):
+        quant(X("PX", 128 * b, 128 * b + 128), X("xb"))
     fill(X("XT"), 0.0)
-    tc(X("NP"), X("IOT", 0, 128))
+    tc(X("NP"), X("JT", 0, 128))
+
+    for h in range(2):
+        act(X("EXP", 512 * h, 512 * h + 512), X("ET"), FN.Copy, off=X("OX", 32 * h, 32 * h + 32))
+        tr(X("ETAB", 512 * h, 512 * h + 512), X("EXP", 512 * h, 512 * h + 512))
+
+    arrive("rq", n - 1, [X("RQIN")])
+    pick(X("SL"), X("XQ"), X("RQIN"))
+    blocks = []
+    for i in range(n - 1):
+        skip = 8 if slot_at(peers[i]) % 2 else 0
+        blocks.append((32 * i + skip, 32 * i + skip + LC))
+    land = (P * me, P * me + LC)
+    each(CODES, [T.SL[:, a:b].bitcast(u8) for a, b in blocks], [T.FW[:, land[0]:land[1]].bitcast(u8) for s in peers], "rc", [X("SL")])
+    each(SCALES, [T.SLS[:, a:b] for a, b in blocks], [T.FWS[:, land[0]:land[1]] for s in peers], "rs", [X("SLS")])
+    for s, w in (("rc", "FW"), ("rs", "FWS")):
+        arrive(s, sum(len(es) for call in CODES for i, es in call), [X(w, 0, 1024)])
+
+    gat(X("E3"), X("ETAB"), X("NBU"))
+    tt(X("E01"), X("E3", 0, 384, 3), X("E3", 1, 384, 3), OP.add)
+    tt(X("E2"), X("E01"), X("E3", 2, 384, 3), OP.add)
+    tt(X("ZS"), X("E2"), X("FB0", 0, 128), OP.add)
+
+    def near_sums():
+        pick(X("PZ", 0, 256), X("NW"), X("LN"))
+        mm("Z", X("UQ"), X("PZ", 0, 128), True, False)
+        mm("Z", X("UQ"), X("PZ", 128, 256), False, False)
 
     c05 = float(np.float32(0.05))
     TINY = 2.0 ** -100
     for t in range(R):
         fw = (1024, 1152, 1280)[t]
-        pick(X("PZ", 256, 384), X("FW", 0, fw), X("LF"))
-        mm("Z", X("UQ"), X("PZ", 256, 384), False, False)
-        mm("Z", X("VQ"), X("BBQ"), False, True)
+        z = X("ZS")
         if t:
+            pick(X("PZ", 256, 384), X("FW", 0, fw), X("LF"))
+            mm("Z", X("UQ"), X("PZ", 256, 384), False, False)
+            mm("Z", X("VQ"), X("BBQ"), False, True)
             tt(X("POS", 512, 768), X("POS", 512, 768), X("UG"), OP.max)
-        z = X("Z", 0, 128)
+            z = X("Z", 0, 128)
         ts(X("NZ"), z, -1.0, OP.mult, TINY, OP.max)
         tt(X("RW"), z, X("NZ"), OP.max)
         tr(X("TR"), X("RW"))
         for k in range(4):
-            act(X("SP", 128 * k, 128 * k + 128), X("CK", 128 * k, 128 * k + 128), FN.Identity, scale=X("TR", 32 * k, 32 * k + 1))
+            act(X("SP", 32 * k, 32 * k + 32), X("CK"), FN.Identity, scale=X("TR", 32 * k, 32 * k + 1))
         for k in range(4):
-            c = X("CM", 128 * k, 128 * k + 128)
-            tt(c, X("RW"), X("SP", 128 * k, 128 * k + 128), OP.is_gt)
-            act(X("JK4", 128 * k, 128 * k + 128), c, FN.Identity, acc=X("CT", k, k + 1))
+            a, b, c = 32 * k, 32 * k + 32, 128 * k
+            val = X("TR", a, a + 1)
+            if b < P:
+                ts(X("CM", c + b, c + P), X("RW", b, P), val, OP.is_gt)
+            if a:
+                ts(X("CM", c, c + a), X("RW", 0, a), val, OP.is_ge)
+            tt(X("CM", c + a, c + b), X("RW", a, b), X("SP", a, b), OP.is_gt)
+            if k < 3:
+                act(X("JK4", c, c + P), X("CM", c, c + P), FN.Identity, acc=X("CT", k, k + 1))
+            else:
+                red(X("CT", k, k + 1), X("CM", c, c + P))
         for k in range(4):
             ts(X("MM", 32 * k, 32 * k + 32), X("IO16"), X("CT", k, k + 1), OP.is_equal, X("LAB", k, k + 1), OP.mult)
         tr(X("MT"), X("MM"))
@@ -418,30 +464,56 @@ def rank_program(g, core, T, topo):
         tc(X("PL"), X("GPT", 0, 128, 32))
         j4 = X("GPT", 96, 97)
         pick(X("PX", 0, 32), X("NW", 0, 128 * (t + 1)), X("PL", 0, 2))
-        pick(X("PX", 32, 48), X("FW", 0, fw), X("PL", 2, 3))
-        for b in range(4):
-            mm("S%d" % b, X("AQ", 128 * b, 128 * b + 128), X("PX"))
-        ts(X("BO", 0, 8, 2), X("IOT", 0, 4), j4, OP.add)
-        ts(X("JU", 0, 1), j4, 0.25, OP.mult)
+        if t == 0:
+            for b in range(4):
+                mm("S%d" % b, X("AQ", 128 * b, 128 * b + 128), X("PX", 0, 128), True, False)
+                mm("S%d" % b, X("AQ", 128 * b, 128 * b + 128), X("PX", 16, 144), False, False)
+        else:
+            pick(X("PX", 32, 48), X("FW", 0, fw), X("PL", 2, 3))
+            for b in range(4):
+                mm("S%d" % b, X("AQ", 128 * b, 128 * b + 128), X("PX", 0, 128))
+        ts(X("BO", 0, 8, 2), X("JT", 0, 4), j4, OP.add)
         for b in range(4):
             act(X("BG", b, 64, 4), X("bbb"), FN.Copy, off=X("BO", 2 * b, 2 * b + 1))
-        sct(X("NP"), X("JU", 0, 1), X("IOT", P * (t + 1), P * (t + 1) + K))
-        if t == 0:
-            tc(X("NLD"), X("PT", 0, 512, 16))
-        if t == R - 1:
-            for d in range(2):
-                tc(X("IDD", d, 16, 2), X("CI"))
-            gat(X("FPD"), X("NP"), X("IDD"))
-            tr(X("FPT"), X("FPD"))
-            tc(X("LFIN"), X("FPT", 0, 256, 32))
-        for b in range(4):
-            act(X("CC", 32 * b, 32 * b + 32), X("S%d" % b, 16, 48), FN.Copy)
-            tt(X("T1", b, 64, 4), X("S%d" % b, 0, 16), X("CC", 32 * b, 32 * b + 16), OP.add)
         if t < R - 1:
+            ts(X("JU", 0, 1), j4, 0.25, OP.mult)
+            sct(X("NP"), X("JU", 0, 1), X("JT", P * (t + 1), P * (t + 1) + K))
+        else:
+            for d in range(2):
+                ts(X("JL", d, d + 1), X("IX"), 16.0 * d, OP.add)
+            sct(X("FPD"), X("JL"), X("VAL"))
+        if t == 0:
+            tr(X("PT"), X("POS", 0, 512))
+            tc(X("NLD"), X("PT", 0, 512, 16))
+            tr(X("FT"), X("POS", 512, 768))
             act(X("POS", 0, 512), X("NP"), FN.Copy, off=X("NLD"))
-        for b in range(4):
-            tt(X("T2", b, 64, 4), X("T1", b, 64, 4), X("CC", 32 * b + 16, 32 * b + 32), OP.add)
-        ts(X("T3"), X("T2"), c05, OP.mult)
+            pick(X("PX", 32, 48), X("FW", 0, fw), X("PL", 2, 3))
+            for b in range(4):
+                mm("S%d" % b, X("AQ", 128 * b, 128 * b + 128), X("PX", 32, 160), False, True)
+            for b in range(4):
+                ts(X("T3", b, 64, 4), X("S%d" % b, 0, 16), c05, OP.mult)
+        else:
+            def one(b):
+                tt(X("T1", b, 64, 4), X("S%d" % b, 0, 16), X("CC", 32 * b, 32 * b + 16), OP.add)
+
+            def two(b):
+                tt(X("T2", b, 64, 4), X("T1", b, 64, 4), X("CC", 32 * b + 16, 32 * b + 32), OP.add)
+            for b in range(4):
+                act(X("CC", 32 * b, 32 * b + 32), X("S%d" % b, 16, 48), FN.Copy)
+            if t < R - 1:
+                act(X("POS", 0, 512), X("NP"), FN.Copy, off=X("NLD"))
+            one(0)
+            one(1)
+            two(0)
+            if t == R - 1:
+                tr(X("FPT"), X("FPD"))
+                tc(X("LFIN"), X("FPT", 0, 256, 32))
+            one(2)
+            two(1)
+            one(3)
+            two(2)
+            two(3)
+            ts(X("T3"), X("T2"), c05, OP.mult)
         tt(X("XT", 0, 64), X("T3"), X("BG"), OP.add)
         new = P * (t + 1)
         quant(X("NW", new, new + 128), X("XT"))
@@ -451,6 +523,7 @@ def rank_program(g, core, T, topo):
             spread(T.NWS[:, new:new + K],
                    [T.FWS[:, fw + K * slot_at(s):fw + K * slot_at(s) + K] for s in peers], "sc%d" % t, [X("NWS", new, new + K)])
             if t == 0:
+                act(X("LBI"), X("LABT"), FN.Copy, off=X("FOU"))
                 act(X("D3"), X("LBI"), FN.Copy, off=X("CIO"))
             tr(X("PT"), X("POS", 0, 512))
             tc(X("LN"), X("PT", 0, 512, 32))
@@ -468,6 +541,11 @@ def rank_program(g, core, T, topo):
                  [X("GP")], [X("NDB", K * t, K * t + K)])
             if t == 0:
                 quant(X("WQ"), X("wb"))
+            else:
+                for d in range(2):
+                    tc(X("IDD", d, 16, 2), X("CI"))
+                gat(X("FPD"), X("NP"), X("IDD"))
+                ts(X("VAL"), X("IO16"), float(P * R), OP.add)
             arrive("cd%d" % t, (n - 1) * bits(shared), [X("FW", fw, fw + 112)])
             arrive("sc%d" % t, (n - 1) * bits(shared), [X("FWS", fw, fw + 112)])
         else:

import numpy as np
from concourse.bass import DstId, RemoteDMATransfer
from concourse.mybir import dt, AluOpType, AxisListType, ActivationFunctionType

F32, I32, U16, B16, Q8, U8 = "float32", "int32", "uint16", "bfloat16", "float8_e4m3fn_x4", "uint8"
P, K, R, LC = 128, 16, 3, 24
SCRATCH = {}
ALIAS = {}


def _sb(kind, **names):
    for k in names:
        SCRATCH[k] = ("sbuf", [128, names[k]], kind)


def _pack(kind, big, **names):
    at = 0
    for k in names:
        ALIAS[k] = (big, at, names[k])
        at += (names[k] + 7) // 8 * 8
    SCRATCH[big] = ("sbuf", [128, at], kind)


_pack(I32, "KI", PID=1, PM16i=1, PM32i=1, W1=1, W2=1, II=32, IO16=32, MJ=16, MJ2=16, MJ3=16, MJ4=16, MJ5=16, CNB=32, MJB=16)
_pack(F32, "KF", PM16=1, PM32=1, PMR=3, MH=3, CI=8, CI128=8, NCI=8, FA=8, FB=8, FC=8, FD0=8, FO=8, GO=8, NGO=8, RS=8, RV=8,
      G8=1, TSH=3, NTAU=8, NPM=1, BASE=8, PC=11, PVC=8, R3=1, LA1=1, LA2=1, LAB=4, CT=4, IX=1, LD=8, PMH=1, BC=4, NVC=4, OFFC=8,
      KJ=32, CKA=32, CKB=32, CK=32, OXF=64, VAL=32)
_pack(U16, "KU", FOU=8, RU=8, PU=24, NBU=24, CN=32, CIO=16, LN=16, NLD=32, FLD=16, LF=8, IDD=16, OFF8=8, PL=4, BO=8, JU=2, OX=64,
      LFIN=8, JL=2)
_sb(I32, NB=24, SF=144, SFL=144, AB=136, VL=256)
_sb(F32, JT=1024, PLK=128, FRF=128, GR=128, JKA=768, JKB=896, CMR=256, NEQ=128, ABF=128, KAP=128, CMP=512, RLD=352, RLT=352, LABT=1024,
    LBI=128, PIO=128, NBR=384, D3=256, POS=1024, PT=512, FT=256, UGT=256, NP=128, UPD=2048, UG=256, LT=256,
    ETR=128, EXP=1024, ETAB=1024, E3=384, E01=128, E2=128, ZS=128,
    NZ=128, RW=128, TR=128, SP=128, CM=512, JK4=512, MM=128, MT=128, GP=128, GPT=128, CC=128, T1=64, T2=64, T3=64,
    NDB=48, FPD=256, FPT=256, YS=128)
_sb(F32, ET=32)
_sb(U16, RQ=12, RQIN=14, GL0=2, GL1=2, RI0=8, RI1=8)
_sb(B16, xb=512, bbb=512, ub=16, vb=16, ab=2048, wb=512, UT=512, VT=512, XT=512, BG=64)
for _n, _w in (("XQ", 128), ("NW", 512), ("BBQ", 128), ("UQ", 128), ("VQ", 128), ("AQ", 512), ("WQ", 128), ("SL", 224), ("FW", 1280),
               ("PZ", 384), ("PX", 256), ("FIN", 128)):
    SCRATCH[_n] = ("sbuf", [128, _w], Q8)
    SCRATCH[_n + "S"] = ("sbuf", [128, _w], U8)
BANKS = ("Z", "S0", "S1", "S2", "S3", "Y", "EB", "FB0")
for _n in BANKS:
    SCRATCH[_n] = ("psum", [128, 512], F32)
SEMAPHORES = ["cv", "cs", "ct", "cp", "ln0", "ln1", "lx", "lb", "lu", "lv", "la", "lw", "ee", "rq", "rc", "rs", "loc",
              "li0", "li1", "cd0", "cd1", "sc0", "sc1", "on", "oc", "os", "oy"]


def rank_program(g, core, T, topo):
    me = T.rank_of(core)
    if me is None:
        return
    n = len(T.cores)
    OP, FN, AX = AluOpType, ActivationFunctionType, AxisListType.X
    E = {"v": g.vector, "s": g.scalar, "t": g.tensor, "p": g, "y": g.sync}
    SEM = {"v": "cv", "s": "cs", "t": "ct", "p": "cp"}
    clock = {e: {} for e in E}
    total, recs = {}, {}

    def norm(x):
        return (x[0], 0, 512, 1) if x[0] in BANKS else x

    def meet(a, b):
        if a[1] >= b[2] or b[1] >= a[2]:
            return False
        return not (a[3] == b[3] and a[3] > 1 and (a[1] - b[1]) % a[3])

    def sync(e, reads, writes):
        toks = []
        for kind, xs in (("r", reads), ("w", writes)):
            for x in xs:
                x = norm(x)
                bank = x[0] in BANKS
                for (y, k, tok, by) in recs.get(x[0], []):
                    if bank and by == e == "t":
                        continue
                    if (kind == "w" or k == "w" or (bank and by != e)) and meet(x, y):
                        toks.append(tok)
        best = {}
        for t in toks:
            if clock[e].get(t[0], 0) < t[1] and best.get(t[0], (0, 0))[1] < t[1]:
                best[t[0]] = t
        for s in sorted(best):
            t = best[s]
            if any(o != s and best[o][2].get(s, 0) >= t[1] for o in best):
                continue
            E[e].wait_ge(T.sem[s], t[1])
        for s in best:
            for k in best[s][2]:
                clock[e][k] = max(clock[e].get(k, 0), best[s][2][k])
            clock[e][s] = max(clock[e].get(s, 0), best[s][1])

    def note(e, tok, reads, writes):
        for x in writes:
            x = norm(x)
            old = recs.setdefault(x[0], [])
            if x[3] == 1 and x[0] not in BANKS:
                old[:] = [r for r in old if not (x[1] <= r[0][1] and r[0][2] <= x[2])]
            old.append((x, "w", tok, e))
        for x in reads:
            x = norm(x)
            recs.setdefault(x[0], []).append((x, "r", tok, e))

    def emit(e, fn, reads, writes):
        reads = [x for x in reads if isinstance(x, tuple)]
        sync(e, reads, writes)
        s = SEM[e]
        total[s] = total.get(s, 0) + 1
        fn().then_inc(T.sem[s], 1)
        snap = dict(clock[e])
        snap[s] = total[s]
        note(e, (s, total[s], snap), reads, writes)

    def dma(q, s, pairs, reads, writes):
        sync(q, reads, writes)
        for o, i in pairs:
            E[q].dma_start(o, i).then_inc(T.sem[s], 16)
        total[s] = 16 * len(pairs)
        snap = dict(clock[q])
        snap[s] = total[s]
        note("d", (s, total[s], snap), reads, writes)

    def arrive(s, val, writes):
        total[s] = val
        note("r", (s, val, {s: val}), [], writes)

    def X(name, lo=0, hi=None, st=1):
        if name in ALIAS:
            big, at, w = ALIAS[name]
            return (big, at + lo, at + (w if hi is None else hi), st)
        return (name, lo, SCRATCH[name][1][1] if hi is None else hi, st)

    def ap(x):
        if not isinstance(x, tuple):
            return x
        return T[x[0]][:, x[1]:x[2]] if x[3] == 1 else T[x[0]][:, x[1]:x[2]:x[3]]

    def sc(x):
        return (x[0] + "S", x[1], x[2], x[3])

    def tt(o, a, b, op):
        emit("v", lambda: g.vector.tensor_tensor(ap(o), ap(a), ap(b), op), [a, b], [o])

    def ts(o, a, s1, op0, s2=None, op1=None):
        if op1 is None:
            emit("v", lambda: g.vector.tensor_scalar(ap(o), ap(a), ap(s1), None, op0), [a, s1], [o])
        else:
            emit("v", lambda: g.vector.tensor_scalar(ap(o), ap(a), ap(s1), ap(s2), op0, op1), [a, s1, s2], [o])

    def tc(o, a):
        emit("v", lambda: g.vector.tensor_copy(ap(o), ap(a)), [a], [o])

    def tr(o, a):
        emit("v", lambda: g.vector.transpose(ap(o), ap(a)), [a], [o])

    def red(o, a):
        emit("v", lambda: g.vector.tensor_reduce(ap(o), ap(a), AX, OP.add), [a], [o])

    def fill(o, c):
        emit("v", lambda: g.vector.memset(ap(o), c), [], [o])

    def gat(o, win, off):
        emit("v", lambda: g.vector.tensor_copy(ap(o), ap(win).indirect(ap(off))), [win, off], [o])

    def sct(win, off, a):
        emit("v", lambda: g.vector.tensor_copy(ap(win).indirect(ap(off)), ap(a)), [a, off], [win])

    def act(o, a, f, bias=None, scale=None, acc=None, off=None):
        kw = {}
        if bias is not None:
            kw["bias"] = ap(bias)
        if scale is not None:
            kw["scale"] = ap(scale)
        if acc is not None:
            kw["accum_out"] = ap(acc)

        def go():
            return g.scalar.activation(ap(o), ap(a) if off is None else ap(a).indirect(ap(off)), f, **kw)
        emit("s", go, [a, bias, scale, off], [o] + ([acc] if acc is not None else []))

    def quant(o, tile):
        emit("v", lambda: g.vector.quantize_mx(ap(o), ap(sc(o)), ap(tile)), [tile], [o, sc(o)])

    def pick(o, win, off):
        emit("v", lambda: g.vector.tensor_copy(ap(o).bitcast(dt.uint32), ap(win).bitcast(dt.uint32).indirect(ap(off))),
             [win, off], [o])
        emit("s", lambda: g.scalar.activation(ap(sc(o)), ap(sc(win)).indirect(ap(off)), FN.Copy), [sc(win), off], [sc(o)])

    def mm(bank, a, b, start=True, stop=True):
        o = (bank, 0, b[2] - b[1], 1)
        emit("t", lambda: g.tensor.matmul_mx(ap(o), ap(a), ap(sc(a)), ap(b), ap(sc(b)), start, stop),
             [a, sc(a), b, sc(b)], [o])

    def iota(o, pattern, cm=0, base=0):
        emit("p", lambda: g.iota(ap(o), pattern, base, cm), [], [o])

    def fiota(o, pattern, base=0):
        emit("p", lambda: g.iota(ap(o), pattern, base, 0, allow_small_or_imprecise_dtypes=True), [], [o])

    peers = [(me + 1 + i) % n for i in range(n - 1)]

    def slot_at(s):
        return (me - s - 1) % n

    def dst(s):
        rid, pid = topo.addr(T.cores[s], core)
        return DstId(rid=rid, pnc=pid)

    shared = topo.mask(core, T.cores[peers[0]])
    for s in peers:
        shared &= topo.mask(core, T.cores[s])

    def bits(m):
        return bin(m).count("1")

    def each(plan, srcs, dsts, sem, reads):
        sync("p", reads, [])
        for call in plan:
            trs = []
            for i, es in call:
                have = topo.engines(core, T.cores[peers[i]])
                m = 0
                for k in es:
                    m |= 1 << have[k]
                trs.append(RemoteDMATransfer(dst_ids=[dst(peers[i])], dma_engine_mask=m, remote_sem=T.sem[sem], src=srcs[i], dst=dsts[i]))
                total["loc"] = total.get("loc", 0) + len(es)
            g.remote_dma_fused(trs, local_sem=T.sem.loc)

    def spread(src, dsts, sem, reads):
        sync("p", reads, [])
        total["loc"] = total.get("loc", 0) + bits(shared)
        g.remote_dma_fused([RemoteDMATransfer(dst_ids=[dst(s) for s in peers], dma_engine_mask=shared, remote_sem=T.sem[sem],
                                              srcs=[src], dsts=dsts)], local_sem=T.sem.loc)

    ONE = [[(i, [i]) for i in range(7)]]
    FOUR = [(i, [2 * i, 2 * i + 1]) for i in range(4)]
    CODES = [FOUR, [(4, [0, 1]), (5, [2, 3]), (6, [4, 5, 6, 7])]]
    SCALES = [FOUR, [(4, [4, 5]), (5, [6, 7]), (6, [0, 1, 2, 3])]]
    u8 = dt.uint8

    for q, s, lo in (("y", "ln0", 0), ("s", "ln1", 4)):
        for k in range(lo, lo + 4):
            E[q].dma_start(T.NB[16 * k:16 * k + 16, :], T.nb[:]).then_inc(T.sem[s], 16)
        total[s] = 64
    recs["NB"] = [(X("NB"), "w", (s, 64, {s: 64}), "d") for s in ("ln0", "ln1")]
    dma("s", "lu", [(T.ub[:], T.u[:, 0:16])], [], [X("ub")])
    dma("y", "lx", [(T.xb[:], T.x[:])], [], [X("xb")])
    dma("s", "lv", [(T.vb[:], T.v[:, 0:16])], [], [X("vb")])
    dma("y", "lb", [(T.bbb[:], T.bb[:])], [], [X("bbb")])
    dma("y", "la", [(T.ab[:], T.a[:])], [], [X("ab")])
    dma("y", "lw", [(T.wb[:], T.w[:])], [], [X("wb")])

    iota(X("PID"), [[0, 1]], 1)
    fiota(X("JT", 0, 256), [[1, 256]])
    iota(X("II"), [[1, 32]])
    fiota(X("OXF"), [[1, 32], [0, 2]])
    wrap = n - 1 - me
    for lo, hi, base in ((0, wrap, -P * (me + 1)), (wrap, 8, 0)):
        if lo < hi and lo % 2:
            fiota(X("BASE", lo, lo + 1), [[0, 1]], base - 8)
            lo, base = lo + 1, base - P
        if hi - lo > 1:
            fiota(X("BASE", lo, hi - hi % 2), [[-2 * P, (hi - lo) // 2], [-P - 8, 2]], base)
        if hi % 2 and lo < hi:
            fiota(X("BASE", hi - 1, hi), [[0, 1]], base - P * (hi - 1 - lo))
    iota(X("CNB"), [[1, 2], [48, 8], [0, 2]])
    iota(X("MJB"), [[48, 8], [0, 2]], 0, 2)
    fiota(X("OFFC"), [[256, 4], [0, 2]])
    fiota(X("KJ"), [[1, 32]])
    fill(X("SF", 0, 8), -1)
    fill(X("SF", 8, 144), 0)
    ts(X("PM16i"), X("PID"), 15, OP.bitwise_and)
    ts(X("PM32i"), X("PID"), 31, OP.bitwise_and)
    ts(X("W1"), X("PM16i"), 11, OP.mult)
    tc(X("PM16"), X("PM16i"))
    for h in range(3):
        ts(X("PMR", h, h + 1), X("PM16i"), float(h - 2), OP.add)
    ts(X("W2"), X("W1"), 5, OP.arith_shift_right)
    ts(X("G8"), X("PM16"), 7.5, OP.is_gt)
    for h in range(3):
        ts(X("MH", h, h + 1), X("W2"), 3.0, OP.mult, X("PMR", h, h + 1), OP.is_equal)
    ts(X("JT", 256, 512), X("JT", 0, 256), 256.0, OP.add)
    ts(X("CI"), X("JT", 0, 128, 16), X("PM16"), OP.add)
    ts(X("PLK"), X("JT", 0, 128), 1.0 / P, OP.mult)
    ts(X("CI128"), X("CI"), 1.0 / P, OP.mult)
    ts(X("NCI"), X("CI"), -1.0 / P, OP.mult)
    ts(X("JT", 512, 1024), X("JT", 0, 512), 512.0, OP.add)
    for b in range(4):
        act(X("UT", b, 512, 4), X("JT", 0, 128), FN.Identity, bias=X("ub", b, b + 1), scale=0.0)

    def shared_column(m):
        ts(X("TSH", m, m + 1), X("G8"), float(P * (peers[2 * m + 1] - peers[2 * m]) - LC), OP.mult, X("PM16"), OP.add)

    for h, o in enumerate(("FA", "FB", "FC")):
        ts(X(o), X("NB", h, 24, 3), X("MH", h, h + 1), OP.mult)
    tt(X("FD0"), X("FA"), X("FB"), OP.add)
    shared_column(0)
    tt(X("FO"), X("FD0"), X("FC"), OP.add)
    shared_column(1)
    tc(X("FOU"), X("FO"))
    tt(X("GO"), X("FO"), X("CI128"), OP.add)
    tt(X("NGO"), X("NCI"), X("FO"), OP.subtract)
    emit("v", lambda: g.vector.tensor_tensor(ap(X("GR")), ap(X("JT")).indirect(ap(X("FOU"))), ap(X("PLK")), OP.add),
         [X("JT"), X("FOU"), X("PLK")], [X("GR")])
    act(X("FRF"), X("JT"), FN.Copy, off=X("FOU"))
    NS = 6
    for t in range(NS):
        act(X("JKA", 128 * t, 128 * t + 128), X("GR"), FN.Sign, bias=X("NGO", t, t + 1), acc=X("RS", t, t + 1))
    quant(X("XQ"), X("xb"))
    quant(X("UQ"), X("UT"))
    mm("EB", X("UQ"), X("XQ"))
    for t in range(NS, 8):
        ts(X("CMR", 128 * (t - NS), 128 * (t - NS) + 128), X("GR"), X("GO", t, t + 1), OP.is_lt)
    tr(X("ETR"), X("EB", 0, 128))
    for t in range(NS, 8):
        red(X("RV", t, t + 1), X("CMR", 128 * (t - NS), 128 * (t - NS) + 128))
    own = X("ET", 4 * me, 4 * me + 4)
    tc(own, X("ETR", 0, 128, 32))
    spread(ap(own), [ap(own) for s in peers], "ee", [own])
    for lo, hi in ((0, 4 * me), (4 * me + 4, 32)):
        if lo < hi:
            arrive("ee", (n - 1) * bits(shared), [X("ET", lo, hi)])
    fiota(X("LABT"), [[32, 64], [1, 16]])
    fiota(X("POS", 768, 1024), [[64, 8], [0, 2], [4, 16]])
    tc(X("RU", NS, 8), X("RV", NS, 8))
    ts(X("RU", 0, NS), X("RS", 0, NS), -0.5, OP.mult, 63.5, OP.add)
    ts(X("NPM"), X("PM16"), -1.0, OP.mult, 0.5, OP.add)
    sct(X("SF", 8, 136), X("RU"), X("FRF"))
    ts(X("NTAU"), X("BASE"), X("NPM"), OP.add)
    ts(X("AB"), X("SF", 8, 144), 896, OP.bitwise_and)
    tt(X("NEQ"), X("SF", 8, 136), X("SF", 7, 135), OP.not_equal)
    tc(X("ABF"), X("AB", 0, 128))
    shared_column(2)
    emit("v", lambda: g.vector.tensor_tensor_scan(ap(X("KAP")), ap(X("NEQ")), ap(X("ABF")), -1.0, OP.add, OP.max),
         [X("NEQ"), X("ABF")], [X("KAP")])
    for i in range(n - 1):
        c = 3 * (i // 2) + 2 * (i % 2)
        act(X("JKB", 128 * i, 128 * i + 128), X("KAP"), FN.Sign, bias=X("NTAU", i, i + 1), acc=X("PC", c, c + 1))
    for m in range(4):
        than = X("TSH", m, m + 1) if m < 3 else X("PM16")
        ts(X("CMP", 128 * m, 128 * m + 128), X("KAP"), P * peers[2 * m] + 16.0, OP.subtract, than, OP.is_lt)
    for m in range(4):
        red(X("PVC", m, m + 1), X("CMP", 128 * m, 128 * m + 128))
    ts(X("SFL", 8, 144), X("SF", 8, 144), 127, OP.bitwise_and)
    ts(X("PC", 1, 11, 3), X("PVC", 0, 4), -2.0, OP.mult, float(P), OP.add)
    for d in range(2):
        ts(X("PU", d, 22, 2), X("PC"), -0.5, OP.mult, 64.0, OP.add)
    gat(X("RLD"), X("SFL", 8, 144), X("PU", 0, 22))
    tr(X("RLT"), X("RLD"))
    tc(X("RQ", 0, 11), X("RLT", 0, 352, 32))
    first = [3 * (i // 2) + i % 2 for i in range(n - 1)]
    each(ONE, [T.RQ[:, c:c + 2] for c in first],
         [T.RQIN[:, 2 * slot_at(s):2 * slot_at(s) + 2] for s in peers], "rq", [X("RQ")])
    fiota(X("UPD"), [[0, 2048]])
    iota(X("VL"), [[1, 256]], 0, 1024)

    tc(X("NBU"), X("NB"))
    tc(X("OX"), X("OXF"))
    ts(X("R3"), X("PM16"), 3.0, OP.mult)
    for i, c in enumerate((2.0 ** -25, 1.0, float(-P * me))):
        fill(X("BC", i, i + 1), c)
    ts(X("CN"), X("CNB"), X("R3"), OP.add)
    ts(X("NVC"), X("vb", 0, 4), -1.0, OP.mult)
    for b in range(4):
        act(X("VT", b, 512, 4), X("JT", 0, 128), FN.Identity, bias=X("NVC", b, b + 1), scale=0.0)
    gat(X("NBR"), X("JT"), X("NBU"))
    act(X("POS", 0, 512), X("NBR"), FN.Identity, bias=X("BC", 2, 3), off=X("CN"))
    ts(X("MJ"), X("MJB"), X("R3"), OP.add)
    quant(X("NW", 0, 128), X("xb"))
    ts(X("MJ2"), X("MJ"), 4, OP.arith_shift_right)
    quant(X("VQ"), X("VT"))
    ts(X("MJ3"), X("MJ2"), 171, OP.mult)
    quant(X("BBQ"), X("bbb"))
    mm("FB0", X("VQ"), X("BBQ"))
    ts(X("MJ4"), X("MJ3"), 9, OP.arith_shift_right)
    ts(X("MJ2"), X("MJ"), 15, OP.bitwise_and)
    ts(X("MJ5"), X("MJ4"), 16, OP.mult)
    tt(X("MJ3"), X("MJ2"), X("MJ5"), OP.add)
    tc(X("CIO"), X("MJ3"))
    act(X("PIO"), X("KAP"), FN.Copy, off=X("RU"))
    act(X("POS", 512, 768), X("PIO"), FN.Copy, off=X("CIO"))
    tc(X("PM32"), X("PM32i"))
    ts(X("PMH"), X("PM32"), -0.5, OP.add)
    act(X("CKA"), X("KJ"), FN.Sign, bias=X("PMH"), scale=-1.0)
    act(X("CKB"), X("CKA"), FN.Identity, bias=X("BC", 0, 1), scale=2.0 ** -25)
    act(X("CK"), X("CKB"), FN.Identity, bias=X("BC", 1, 2), scale=-1.0)
    ts(X("LA1"), X("PM32"), 16.0, OP.is_ge, 16.0, OP.mult)
    ts(X("IO16"), X("II"), 15, OP.bitwise_and)
    tt(X("LA2"), X("LA1"), X("PM32"), OP.add)
    for b in range(4):
        quant(X("AQ", 128 * b, 128 * b + 128), X("ab", 512 * b, 512 * b + 512))
    ts(X("LAB"), X("JT", 0, 256, 64), X("LA2"), OP.add)
    for b in range(2):
        quant(X("PX", 128 * b, 128 * b + 128), X("xb"))
    fill(X("XT"), 0.0)
    tc(X("NP"), X("JT", 0, 128))

    for h in range(2):
        act(X("EXP", 512 * h, 512 * h + 512), X("ET"), FN.Copy, off=X("OX", 32 * h, 32 * h + 32))
        tr(X("ETAB", 512 * h, 512 * h + 512), X("EXP", 512 * h, 512 * h + 512))

    arrive("rq", n - 1, [X("RQIN")])
    pick(X("SL"), X("XQ"), X("RQIN"))
    blocks = []
    for i in range(n - 1):
        skip = 8 if slot_at(peers[i]) % 2 else 0
        blocks.append((32 * i + skip, 32 * i + skip + LC))
    land = (P * me, P * me + LC)
    each(CODES, [T.SL[:, a:b].bitcast(u8) for a, b in blocks], [T.FW[:, land[0]:land[1]].bitcast(u8) for s in peers], "rc", [X("SL")])
    each(SCALES, [T.SLS[:, a:b] for a, b in blocks], [T.FWS[:, land[0]:land[1]] for s in peers], "rs", [X("SLS")])
    for s, w in (("rc", "FW"), ("rs", "FWS")):
        arrive(s, sum(len(es) for call in CODES for i, es in call), [X(w, 0, 1024)])

    gat(X("E3"), X("ETAB"), X("NBU"))
    tt(X("E01"), X("E3", 0, 384, 3), X("E3", 1, 384, 3), OP.add)
    tt(X("E2"), X("E01"), X("E3", 2, 384, 3), OP.add)
    tt(X("ZS"), X("E2"), X("FB0", 0, 128), OP.add)

    def near_sums():
        pick(X("PZ", 0, 256), X("NW"), X("LN"))
        mm("Z", X("UQ"), X("PZ", 0, 128), True, False)
        mm("Z", X("UQ"), X("PZ", 128, 256), False, False)

    c05 = float(np.float32(0.05))
    TINY = 2.0 ** -100
    for t in range(R):
        fw = (1024, 1152, 1280)[t]
        z = X("ZS")
        if t:
            pick(X("PZ", 256, 384), X("FW", 0, fw), X("LF"))
            mm("Z", X("UQ"), X("PZ", 256, 384), False, False)
            mm("Z", X("VQ"), X("BBQ"), False, True)
            tt(X("POS", 512, 768), X("POS", 512, 768), X("UG"), OP.max)
            z = X("Z", 0, 128)
        ts(X("NZ"), z, -1.0, OP.mult, TINY, OP.max)
        tt(X("RW"), z, X("NZ"), OP.max)
        tr(X("TR"), X("RW"))
        for k in range(4):
            act(X("SP", 32 * k, 32 * k + 32), X("CK"), FN.Identity, scale=X("TR", 32 * k, 32 * k + 1))
        for k in range(4):
            a, b, c = 32 * k, 32 * k + 32, 128 * k
            val = X("TR", a, a + 1)
            if b < P:
                ts(X("CM", c + b, c + P), X("RW", b, P), val, OP.is_gt)
            if a:
                ts(X("CM", c, c + a), X("RW", 0, a), val, OP.is_ge)
            tt(X("CM", c + a, c + b), X("RW", a, b), X("SP", a, b), OP.is_gt)
            if k < 3:
                act(X("JK4", c, c + P), X("CM", c, c + P), FN.Identity, acc=X("CT", k, k + 1))
            else:
                red(X("CT", k, k + 1), X("CM", c, c + P))
        for k in range(4):
            ts(X("MM", 32 * k, 32 * k + 32), X("IO16"), X("CT", k, k + 1), OP.is_equal, X("LAB", k, k + 1), OP.mult)
        tr(X("MT"), X("MM"))
        red(X("IX"), X("MT"))
        ts(X("OFF8"), X("OFFC"), X("IX"), OP.add)
        if t < R - 1:
            gl = "GL%d" % t
            ts(X(gl, 0, 1), X("IX"), 256.0 * me, OP.add)
            spread(T[gl][:, 0:1], [T["RI%d" % t][:, slot_at(s):slot_at(s) + 1] for s in peers], "li%d" % t, [X(gl, 0, 1)])
        gat(X("GP"), X("POS"), X("OFF8"))
        tr(X("GPT"), X("GP"))
        tc(X("PL"), X("GPT", 0, 128, 32))
        j4 = X("GPT", 96, 97)
        pick(X("PX", 0, 32), X("NW", 0, 128 * (t + 1)), X("PL", 0, 2))
        if t == 0:
            for b in range(4):
                mm("S%d" % b, X("AQ", 128 * b, 128 * b + 128), X("PX", 0, 128), True, False)
                mm("S%d" % b, X("AQ", 128 * b, 128 * b + 128), X("PX", 16, 144), False, False)
        else:
            pick(X("PX", 32, 48), X("FW", 0, fw), X("PL", 2, 3))
            for b in range(4):
                mm("S%d" % b, X("AQ", 128 * b, 128 * b + 128), X("PX", 0, 128))
        ts(X("BO", 0, 8, 2), X("JT", 0, 4), j4, OP.add)
        for b in range(4):
            act(X("BG", b, 64, 4), X("bbb"), FN.Copy, off=X("BO", 2 * b, 2 * b + 1))
        if t < R - 1:
            ts(X("JU", 0, 1), j4, 0.25, OP.mult)
            sct(X("NP"), X("JU", 0, 1), X("JT", P * (t + 1), P * (t + 1) + K))
        else:
            for d in range(2):
                ts(X("JL", d, d + 1), X("IX"), 16.0 * d, OP.add)
            sct(X("FPD"), X("JL"), X("VAL"))
        if t == 0:
            tr(X("PT"), X("POS", 0, 512))
            tc(X("NLD"), X("PT", 0, 512, 16))
            tr(X("FT"), X("POS", 512, 768))
            act(X("POS", 0, 512), X("NP"), FN.Copy, off=X("NLD"))
            pick(X("PX", 32, 48), X("FW", 0, fw), X("PL", 2, 3))
            for b in range(4):
                mm("S%d" % b, X("AQ", 128 * b, 128 * b + 128), X("PX", 32, 160), False, True)
            for b in range(4):
                ts(X("T3", b, 64, 4), X("S%d" % b, 0, 16), c05, OP.mult)
        else:
            def one(b):
                tt(X("T1", b, 64, 4), X("S%d" % b, 0, 16), X("CC", 32 * b, 32 * b + 16), OP.add)

            def two(b):
                tt(X("T2", b, 64, 4), X("T1", b, 64, 4), X("CC", 32 * b + 16, 32 * b + 32), OP.add)
            for b in range(4):
                act(X("CC", 32 * b, 32 * b + 32), X("S%d" % b, 16, 48), FN.Copy)
            if t < R - 1:
                act(X("POS", 0, 512), X("NP"), FN.Copy, off=X("NLD"))
            one(0)
            one(1)
            two(0)
            if t == R - 1:
                tr(X("FPT"), X("FPD"))
                tc(X("LFIN"), X("FPT", 0, 256, 32))
            one(2)
            two(1)
            one(3)
            two(2)
            two(3)
            ts(X("T3"), X("T2"), c05, OP.mult)
        tt(X("XT", 0, 64), X("T3"), X("BG"), OP.add)
        new = P * (t + 1)
        quant(X("NW", new, new + 128), X("XT"))
        if t < R - 1:
            spread(T.NW[:, new:new + K].bitcast(u8),
                   [T.FW[:, fw + K * slot_at(s):fw + K * slot_at(s) + K].bitcast(u8) for s in peers], "cd%d" % t, [X("NW", new, new + K)])
            spread(T.NWS[:, new:new + K],
                   [T.FWS[:, fw + K * slot_at(s):fw + K * slot_at(s) + K] for s in peers], "sc%d" % t, [X("NWS", new, new + K)])
            if t == 0:
                act(X("LBI"), X("LABT"), FN.Copy, off=X("FOU"))
                act(X("D3"), X("LBI"), FN.Copy, off=X("CIO"))
            tr(X("PT"), X("POS", 0, 512))
            tc(X("LN"), X("PT", 0, 512, 32))
            near_sums()
            if t == 0:
                tr(X("LT"), X("D3"))
                tc(X("FLD"), X("LT", 0, 256, 16))
            arrive("li%d" % t, (n - 1) * bits(shared), [X("RI%d" % t, 0, 7)])
            sct(X("UPD"), X("RI%d" % t, 0, 7), X("VL", fw - 1024, fw - 1024 + 112))
            gat(X("UG"), X("UPD"), X("FLD"))
            tr(X("UGT"), X("UG"))
            tt(X("LD"), X("FT", 0, 256, 32), X("UGT", 0, 256, 32), OP.max)
            tc(X("LF"), X("LD"))
            emit("v", lambda: g.vector.tensor_scalar(T.NDB[0:1, K * t:K * t + K], T.GP[0:1, 96:112], 0.25, None, OP.mult),
                 [X("GP")], [X("NDB", K * t, K * t + K)])
            if t == 0:
                quant(X("WQ"), X("wb"))
            else:
                for d in range(2):
                    tc(X("IDD", d, 16, 2), X("CI"))
                gat(X("FPD"), X("NP"), X("IDD"))
                ts(X("VAL"), X("IO16"), float(P * R), OP.add)
            arrive("cd%d" % t, (n - 1) * bits(shared), [X("FW", fw, fw + 112)])
            arrive("sc%d" % t, (n - 1) * bits(shared), [X("FWS", fw, fw + 112)])
        else:
            pick(X("FIN"), X("NW"), X("LFIN"))
            mm("Y", X("WQ"), X("FIN"))
            dma("y", "oc", [(T.oc[:], T.FIN[:].bitcast(u8))], [X("FIN")], [])
            dma("y", "os", [(T.osc[4 * k:4 * k + 4, :], T.FINS[32 * k:32 * k + 4, :]) for k in range(4)], [X("FINS")], [])
            tc(X("YS"), X("Y", 0, 128))
            dma("s", "oy", [(T.y[:], T.YS[:])], [X("YS")], [])
            emit("v", lambda: g.vector.tensor_scalar(T.NDB[0:1, K * t:K * t + K], T.GP[0:1, 96:112], 0.25, None, OP.mult),
                 [X("GP")], [X("NDB", K * t, K * t + K)])
            dma("s", "on", [(T.nd[:], T.NDB[0:1, :])], [X("NDB")], [])
    for s in total:
        if clock["p"].get(s, 0) < total[s]:
            g.wait_ge(T.sem[s], total[s])
